import numpy as np, ml_dtypes
CORES = [10,34,74,98]
N = 4
import mx_ref
BF = ml_dtypes.bfloat16
def gcols(t, e):
    v = np.concatenate([t.reshape(8, 16, -1, 4), np.zeros((8, 16, 1, 4), BF)], axis=2)
    return np.ascontiguousarray(np.stack([v[g][:, e[g]] for g in range(8)])).reshape(128, -1)
def tile(rs):
    return np.stack(rs, axis=2).reshape(128, -1).astype(BF)
def cut(t, i, w=512):
    return t[:, w * i:w * i + w]
def pick(q, e):
    c = np.concatenate([q[0].reshape(128, -1, 4), np.zeros((128, 1, 4), np.uint8)], axis=1); s = np.concatenate([q[1], np.ones((16, 1), np.uint8)], axis=1)
    return (np.ascontiguousarray(c[:, e].reshape(128, -1)), np.ascontiguousarray(s[:, e]))
def join(*qs):
    return (np.concatenate([q[0] for q in qs], axis=1), np.concatenate([q[1] for q in qs], axis=1))
def put(q, e, v):
    c, s = q[0].reshape(128, -1, 4).copy(), q[1].copy(); c[:, e] = v[0].reshape(128, -1, 4); s[:, e] = v[1]
    return (c.reshape(128, -1), s)
def pk(c, s):
    return (np.ascontiguousarray(c), mx_ref.live(s))
def emit(q):
    return q[0], q[1]
def packed(v, rng):
    q = [mx_ref.quantize(np.ascontiguousarray(v[r])) for r in range(N)]
    return np.stack([a for a, b in q]), np.stack([mx_ref.plane(b, rng) for a, b in q])
def values_of_codes():
    e, c = np.zeros((128, 128, 4), np.float32), np.zeros((128, 2, 4), np.uint8)
    e[np.arange(128), np.arange(128), 0] = 1
    c[:127, :, 0] = np.arange(256).reshape(2, 128).T[:127]
    return mx_ref.matmul(mx_ref.quantize(e.reshape(128, 512).astype(BF)), (c.reshape(128, 8), np.full((16, 2), 127, np.uint8))).T.reshape(-1).astype(np.float64)
CODE_VALUE, SCALE_VALUE = values_of_codes(), 2.0 ** (np.arange(256) - 127.0)
def decode(q):
    return (CODE_VALUE[q[0]].reshape(16, 8, -1, 4) * SCALE_VALUE[q[1]][:, None, :, None] + 0.0).reshape(128, -1).astype(np.float32)
def f(rng, *shape):
    return mx_ref.flush((rng.standard_normal(shape, dtype=np.float32) * np.exp2(rng.integers(-2, 3, shape[:-1] + (1,)))).astype(BF))
def wide(rng, *shape, cols=0):
    v = rng.standard_normal(shape, dtype=np.float32) * np.exp2(rng.integers(-12, 13, shape)).astype(np.float32)
    if cols: v *= np.repeat(np.exp2(rng.integers(-cols, cols + 1, shape[:-2] + (1, shape[-1] // 4))) * (rng.random(shape[:-2] + (1, shape[-1] // 4)) > 0.0625), 4, axis=-1).astype(np.float32)
    return mx_ref.flush(v.astype(BF))
C, A, K, R = 320, 96, 128, 3
STEP = [1, 2, 3]
def order(p):
    return np.argsort(-(p[::16] + np.float32(0.0)), axis=1, kind="stable")
def gput(t, e, h):
    a, b = t.reshape(8, 16, -1, 4).copy(), h.reshape(8, 16, -1, 4)
    for g in range(8): a[g][:, e[g]] = b[g]
    return a.reshape(128, -1)
def parts(m):
    return np.repeat(np.repeat(m, 16, axis=0), 4, axis=1)
def big(v):
    v = v.astype(np.float32)
    v[np.abs(v) < np.float32(2.0 ** -16)] = 0
    return v.astype(BF)
def numbers_of(rng):
    return {"x": big(f(rng, N, 128, 4 * C)), "u": np.array(f(rng, N, 128, 512)), "v": np.array(f(rng, N, 128, 512))}
def layers(rng):
    return big(f(rng, N, 128, 2048)).reshape(N, 8, 16, 4, 8, 16, 4)
def weights(rng, w):
    c, p = packed(np.ascontiguousarray(w).reshape(N, 128, 2048), rng)
    return {"wc": c, "ws": p}
def signs(rng):
    return np.stack([rng.permutation(8) % 2 * 2.0 - 1.0 for r in range(N)])
def setup_inputs(rng):
    return {**numbers_of(rng), **weights(rng, layers(rng))}
def setup_inputs_ties(rng):
    d = numbers_of(rng)
    e = rng.permutation(N)
    x = d["x"].reshape(N, 8, 16, C, 4)
    for r in range(N):
        k = np.zeros(C, int) if r == e[0] else rng.permutation(C) % 3
        a = x[r][:, :8, :3].copy()
        a[:, :, 2] = 0
        x[r][:, :8] = a[:, :, k]
    x[e[1]] = 0
    u = d["u"].reshape(N, 8, 16, 128, 4)
    u[:, :, 8:, ::16] = 0
    w = layers(rng)
    w[:, :, 8:, :, :, :8] = 0
    return {"x": x.reshape(N, 128, 4 * C), "u": u.reshape(N, 128, 512), "v": d["v"], **weights(rng, w)}
def setup_inputs_near(rng):
    d = numbers_of(rng)
    x = np.zeros((N, 8, 16, C, 4), np.float32)
    u = d["u"].reshape(N, 128, 128, 4)
    u[:, :, ::16] = 0
    o, c = rng.permutation(N) % 4, signs(rng)
    upper = np.arange(C) // (C // 2)
    for r in range(N):
        i = (np.arange(C) + rng.integers(0, C, (8, 1))) % C
        if o[r] == 3: i = i % (C // 2) * 2 + upper
        s = (i + 1) // 2
        size = 1.0 if o[r] < 2 else 2.0 ** -4
        g = ((s[:, :, None] >> np.arange(8)) & 1) * np.exp2(np.arange(8) - 23.0) * size
        if o[r] < 2: x[r, :, 0, :, 0] = c[r][:, None]
        if o[r] == 3: x[r, :, 0, :, 0] = (8 + upper) * 2.0 ** -30
        x[r, :, 8] = g[:, :, :4]
        x[r, :, 9] = g[:, :, 4:]
        x[r, :, 10:] = rng.integers(4, 8, (8, 6, C, 4)) * 2.0 ** -20 * size
        k = 1.0 if o[r] == 0 else 2.0 ** -30
        for h in range(0, 128, 16):
            u[r, h, h, 0] = k
            u[r, h + 8:h + 10, h] = k
    w = layers(rng)
    w[:, :, :10] = 0
    w[:, :, :, :, :, :10] = 0
    return {"x": x.reshape(N, 128, 4 * C).astype(BF), "u": u.reshape(N, 128, 512), "v": d["v"], **weights(rng, w)}
def setup_inputs_huge(rng):
    d = numbers_of(rng)
    c = np.stack([rng.permutation(C) % 2 * 2.0 - 1.0 for r in range(N)])
    c[rng.permutation(N) < N // 2] = -1
    x = (0.6 + 0.2 * rng.random((N, 128, C, 4))) * np.where(c < 0, -2.0 ** 30, 2.0 ** 28)[:, None, :, None]
    u = d["u"].reshape(N, 128, 128, 4)
    a = 2.0 ** 30 * (1 - 0.25 * rng.random((N, 128, 8, 4))) * signs(rng)[:, None, :, None]
    u[:, :, ::16] = a.astype(np.float32).astype(BF)
    w = np.zeros((N, 128, 4, 128, 4), np.float32)
    i = np.arange(128)
    for b in range(4): w[:, i, b, i, b] = 16
    return {"x": x.astype(np.float32).reshape(N, 128, 4 * C).astype(BF), "u": u.reshape(N, 128, 512), "v": d["v"], **weights(rng, w.astype(BF))}
def setup_inputs_slots(rng):
    d = numbers_of(rng)
    s = np.zeros((N, 8, C), bool)
    h = int(rng.integers(8))
    for r in range(N):
        p = r ^ STEP[0]
        if r < p:
            n = rng.permutation(np.array([K, K - 1, K + 1, 2 * A, A, rng.integers(A, 2 * A + 1), rng.integers(A, 2 * A + 1)]))
            n = np.insert(n, h, A)
            for g in range(8):
                e = rng.permutation(C)
                s[r, g, e[:A]] = True
                s[p, g, e[n[g] - A:n[g]]] = True
    s[:, h] = np.isin(np.arange(C), rng.permutation(C)[:A])
    k = (s * rng.integers(8, 16, (N, 8, C)) * 0.125).astype(np.float32).astype(BF)
    x = d["x"].reshape(N, 8, 16, C, 4)
    x[:, :, :8] = 0
    u = d["u"].reshape(N, 128, 128, 4)
    u[:, :, ::16] = 0
    for r in range(N):
        x[:, :, r, :, 0] = k[r]
        for g in range(8): u[r, 16 * g + r, 16 * g, 0] = 1
    w = layers(rng)
    w[:, :, :, :, :, :8] = 0
    return {"x": x.reshape(N, 128, 4 * C), "u": u.reshape(N, 128, 512), "v": d["v"], **weights(rng, w)}
def setup_inputs_spread(rng):
    d = setup_inputs(rng)
    d["x"] = big(wide(rng, N, 128, 4 * C, cols=6))
    return d
def check_inputs(d):
    b = []
    for k in ("x", "u", "v"):
        a = np.abs(d[k].astype(np.float32))
        if not (np.isfinite(a).all() and ((a == 0) | (a >= 2.0 ** -30) & (a <= 2.0 ** 30)).all()): b.append("a value of " + k)
    none, least, most = [emit(mx_ref.quantize(np.full((128, 16), k, np.float32).astype(BF)))[1][0, 0] for k in (0.0, 2.0 ** -30, 2.0 ** 30)]
    for r in range(N):
        if ((d["wc"][r] == 0x7F) | (d["wc"][r] == 0xFF)).any(): b.append("wc: a code that is no number")
        s = mx_ref.live(d["ws"][r])
        if ((s != none) & ((s < least) | (s > most))).any(): b.append("ws: a scale out of range")
    return b
def reference(x, u, v, wc, ws):
    qu = [mx_ref.quantize(u[r]) for r in range(N)]
    lay = [pk(wc[r], ws[r]) for r in range(N)]
    now = [x[r] for r in range(N)]
    vec = np.zeros((N, 8, C, N), np.int64)
    for t in range(R):
        sent = []
        for r in range(N):
            e = order(mx_ref.matmul(qu[r], mx_ref.quantize(now[r])))[:, :A]
            z = gcols(now[r], e)
            q = mx_ref.quantize(z)
            h = tile([np.maximum(mx_ref.matmul(pick(lay[r], np.arange(128 * b, 128 * b + 128)), q), np.float32(0.0)) * np.float32(0.03125) + z[:, b::4].astype(np.float32) for b in range(4)])
            now[r] = gput(now[r], e, h)
            for g in range(8): vec[r, g, e[g], r] += 1
            sent.append(mx_ref.quantize(now[r]))
        came = decode(join(*sent)).astype(BF)
        had = vec.copy()
        for r in range(N):
            p = r ^ STEP[t]
            want = (had[p] > had[r]).any(axis=2)
            for g in range(8): want[g, np.flatnonzero(want[g])[K:]] = False
            newer = (had[p] >= had[r]).all(axis=2)
            c = cut(came, p, 4 * C)
            half = ((now[r].astype(np.float32) + c.astype(np.float32)) * np.float32(0.5)).astype(BF)
            new = now[r].copy()
            a, b = parts(want & newer), parts(want & ~newer)
            new[a] = c[a]
            new[b] = half[b]
            now[r] = new
            vec[r][want] = np.maximum(had[r], had[p])[want]
    y, ov = np.zeros((N, 128, C), np.float32), np.zeros((N, 8, C), np.float32)
    oc, osc = np.zeros((N, 128, 4 * C), np.uint8), np.zeros((N, 16, C), np.uint8)
    for r in range(N):
        q = mx_ref.quantize(now[r])
        y[r] = mx_ref.matmul(mx_ref.quantize(v[r]), q)
        ov[r] = np.sum(vec[r] * 4 ** np.arange(N), axis=2)
        oc[r], osc[r] = emit(q)
    return {"y": y, "ov": ov, "oc": oc, "osc": osc}

@@ -1,0 +1,452 @@
+import numpy as np
+from concourse.mybir import dt, AluOpType as Op, ActivationFunctionType as Fn
+
+C, A, K, R = 320, 96, 128, 3
+STEP = [1, 2, 3]
+NV = 11
+CUTS = [10, 20]
+WH, WX, WDO, WAO, WEND = 0, 96, 416, 736, 1248
+BIG = 4096.0
+
+F, B, U, I, Q, S = "float32", "bfloat16", "uint16", "int32", "float8_e4m3fn_x4", "uint8"
+SCRATCH = {}
+
+
+def _buf(name, n, d, where="sbuf"):
+    SCRATCH[name] = (where, [128, n], d)
+
+
+for _t in range(R):
+    _buf("win%d" % _t, 4 * WEND, B)
+    _buf("qx%d" % _t, C, Q); _buf("sx%d" % _t, C, S)
+    _buf("qh%d" % _t, 128, Q); _buf("sh%d" % _t, 128, S)
+    _buf("lq%d" % _t, A + C, Q); _buf("ls%d" % _t, A + C, S)
+    _buf("eo%d" % _t, 24, U); _buf("le%d" % _t, 24, U); _buf("rk%d" % _t, 20, U); _buf("lr%d" % _t, 20, U)
+_buf("win3", 4 * (WX + C), B); _buf("qx3", C, Q); _buf("sx3", C, S)
+_buf("pre1", 20, U); _buf("lp1", 20, U); _buf("pre2", 80, U); _buf("lp2", 80, U)
+for _n in "uv":
+    _buf(_n + "t", 512, B); _buf("q" + _n, 128, Q); _buf("s" + _n, 128, S)
+_buf("qup", 128, Q); _buf("sup", 128, S)
+_buf("qw", 512, Q); _buf("sw", 512, S)
+_buf("half", 512, B); _buf("et", 2048, B); _buf("qe", 512, Q); _buf("se", 512, S)
+_buf("z", 512, B); _buf("qz", 128, Q); _buf("sz", 128, S)
+_buf("rl", 4 * A, F); _buf("xh", 4 * C, B); _buf("own", 4 * A, B); _buf("yo", C, F)
+for _b in range(8):
+    _buf("ps%d" % _b, 512, F, "psum")
+_buf("pi", 4, I); _buf("pf", 8, F); _buf("oui", 8, I); _buf("ou", 8, U)
+_buf("m16", C, F); _buf("mask", C, B); _buf("nmask", C, B); _buf("kc", 20, F)
+_buf("c4", C, F); _buf("cval", C, F); _buf("l16", 20, F); _buf("cx", 20, F); _buf("cdo", 20, F); _buf("c2", 20, F)
+_buf("m4", 240, F); _buf("pa", A, F); _buf("pb", A, F); _buf("pat", A, F); _buf("rs", 240, F); _buf("iow", 256, B)
+_buf("mm", C, F); _buf("hd", C, F); _buf("eq", C, B); _buf("nc", C, B); _buf("ini", 20, B)
+_buf("fl", NV * C, B); _buf("cum", NV * 160, B); _buf("sg", (20 - NV) * C, B); _buf("junk", C, B)
+_buf("a1", 20, F); _buf("a2", 20, F); _buf("e", C, F); _buf("es", A, F)
+_buf("moff", 80, U); _buf("foff", 80, U); _buf("wu", 20, U); _buf("wrow", C, B); _buf("wcum", C, B); _buf("acc", 2, F)
+_buf("sm", 40 * 20, F)
+_buf("pd", 80, F); _buf("dd", 80, F); _buf("gl", 240, F); _buf("gs", 240, F); _buf("ovu", 20, U); _buf("ovr", C, F)
+
+SEMAPHORES = ["cv", "cs", "ct", "cg", "lx", "lu", "lw", "lws", "lv", "out", "sent", "ap1", "ap2", "ao1", "ao2"] + \
+    ["%s%d" % (n, t) for t in range(R) for n in ("ae", "ar", "ah")]
+
+
+def rank_program(g, core, T, topo):
+    r = T.rank_of(core)
+    if r is None:
+        return
+    queues = {"v": g.vector, "s": g.scalar, "t": g.tensor, "g": g, "y": g.sync}
+    ops, last_w, last_r, seq, sent, stored = [], {}, {}, {}, [0], [0]
+
+    def V(name, lo=0, hi=None, step=1):
+        n = SCRATCH[name][1][1]
+        hi = n if hi is None else hi
+        ap = T[name][:, lo:hi] if step == 1 else T[name][:, lo:hi:step]
+        cols = np.arange(n) if name.startswith("ps") else np.arange(lo, hi, step)
+        return {"ap": ap, "at": [(name, cols)], "also": []}
+
+    def ind(win, off, words=False):
+        ap = win["ap"].bitcast(dt.uint32) if words else win["ap"]
+        return {"ap": ap.indirect(off["ap"]), "at": win["at"], "also": off["at"]}
+
+    def ap(x):
+        return x["ap"] if isinstance(x, dict) else x
+
+    def add(q, fn, reads, writes, stream=None, token=None):
+        me = len(ops)
+        stream = stream or q
+        rd = [a for x in reads if isinstance(x, dict) for a in x["at"] + x["also"]] + [a for x in writes for a in x["also"]]
+        wr = [a for x in writes for a in x["at"]]
+        deps = set()
+        for name, cols in rd + wr:
+            if name not in last_w:
+                last_w[name] = np.full(SCRATCH[name][1][1], -1)
+                last_r[name] = {}
+            deps.update(int(d) for d in np.unique(last_w[name][cols]))
+        for name, cols in wr + [a for a in rd if a[0].startswith("ps")]:
+            for s, a in last_r[name].items():
+                if s != stream:
+                    deps.update(int(d) for d in np.unique(a[cols]))
+        deps.discard(-1)
+        for name, cols in rd:
+            last_r[name].setdefault(stream, np.full(SCRATCH[name][1][1], -1))[cols] = me
+        for name, cols in wr:
+            last_w[name][cols] = me
+        seq[stream] = seq.get(stream, -1) + 1
+        ops.append({"q": q, "fn": fn, "deps": deps, "stream": stream, "seq": seq[stream], "token": token, "waits": [], "need": False})
+
+    def tt(o, a, b, op): add("v", lambda: g.vector.tensor_tensor(ap(o), ap(a), ap(b), op), [a, b], [o])
+    def cp(o, a): add("v", lambda: g.vector.tensor_copy(ap(o), ap(a)), [a], [o])
+    def ms(o, c): add("v", lambda: g.vector.memset(ap(o), c), [], [o])
+    def scan(o, a, b, ini, o0, o1): add("v", lambda: g.vector.tensor_tensor_scan(ap(o), ap(a), ap(b), ap(ini), o0, o1), [a, b, ini], [o])
+    def quant(q, s, a): add("v", lambda: g.vector.quantize_mx(ap(q), ap(s), ap(a)), [a], [q, s])
+
+    def ts(o, a, s1, o0, s2=None, o1=None):
+        if o1 is None:
+            add("v", lambda: g.vector.tensor_scalar(ap(o), ap(a), ap(s1), None, o0), [a, s1], [o])
+        else:
+            add("v", lambda: g.vector.tensor_scalar(ap(o), ap(a), ap(s1), ap(s2), o0, o1), [a, s1, s2], [o])
+
+    def act(o, a, fn, bias=None, scale=None, acc=None):
+        kw = {}
+        if bias is not None: kw["bias"] = ap(bias)
+        if scale is not None: kw["scale"] = ap(scale)
+        if acc is not None: kw["accum_out"] = ap(acc)
+        add("s", lambda: g.scalar.activation(ap(o), ap(a), fn, **kw), [a, bias, scale], [o] + ([acc] if acc else []))
+
+    def mm(o, n, lq, ls, rq, rs):
+        add("t", lambda: g.tensor.matmul_mx(T[o][:, 0:n], ap(lq), ap(ls), ap(rq), ap(rs), True, True), [lq, ls, rq, rs], [V(o)])
+
+    def iota(o, pat, base, cm=0, flag=True):
+        if flag:
+            add("g", lambda: g.iota(ap(o), pat, base, cm, allow_small_or_imprecise_dtypes=True), [], [o])
+        else:
+            add("g", lambda: g.iota(ap(o), pat, base, cm), [], [o])
+
+    def load(q, o, oap, src, sem, after=()):
+        add(q, lambda: queues[q].dma_start(oap, src).then_inc(T.sem[sem], 16), list(after), [o], stream=sem, token=(sem, 16))
+
+    def store(q, dst, a, aap):
+        stored[0] += 16
+        add(q, lambda: queues[q].dma_start(dst, aap).then_inc(T.sem.out, 16), [a], [], stream="st%d" % stored[0], token=("out", 0))
+
+    def send(peer, o, a, sem, codes=False):
+        dst = T.cores[peer]
+        rid, pid = topo.addr(dst)[0:2]
+        sent[0] += len(topo.engines(core, dst))
+        oa, aa = (o["ap"].bitcast(dt.uint8), a["ap"].bitcast(dt.uint8)) if codes else (o["ap"], a["ap"])
+        add("g", lambda: g.remote_dma(oa, aa, T.sem[sem], T.sem.sent, pid, rid, topo.mask(core, dst)), [a], [],
+            stream="rd%d" % sent[0], token=("sent", 0))
+
+    def arrive(peer, views, sem):
+        add(None, None, [], views, stream=sem, token=(sem, len(views) * len(topo.engines(T.cores[peer], core))))
+
+    slots = {}
+
+    def L(name):
+        k = slots.setdefault(name, len(slots))
+        return V("sm", 20 * k, 20 * k + 20)
+
+    def W(t, lo, hi, b=None):
+        return V("win%d" % t, 4 * lo, 4 * hi) if b is None else V("win%d" % t, 4 * lo + b, 4 * hi, 4)
+
+    def digit(i):
+        return V("gl", 160 + i, 240, 4)
+
+    def E(b):
+        return V("qe", 128 * b, 128 * b + 128), V("se", 128 * b, 128 * b + 128)
+
+    load("y", W(0, WX, WX + C), W(0, WX, WX + C)["ap"], T.x[:], "lx")
+    load("s", V("ut"), T.ut[:], T.u[:], "lu")
+    load("y", V("qw"), T.qw[:].bitcast(dt.uint8), T.wc[:], "lw", [W(0, WX, WX + C)])
+    load("y", V("sw"), T.sw[:], T.ws[:], "lws")
+    load("y", V("vt"), T.vt[:], T.v[:], "lv")
+    iota(V("pi", 0, 1), [[0, 1]], 0, 1, False)
+    iota(V("oui"), [[16, 8]], 0, 0, False)
+    iota(V("m16"), [[0, 20], [1, 16]], 0)
+    iota(V("m4"), [[0, 60], [1, 4]], 0)
+    iota(V("kc", 0, NV), [[0, NV]], -160)
+    iota(V("kc", NV, 20), [[16, 20 - NV]], 16 * NV + 16 - 160)
+    iota(V("l16"), [[16, 20]], WX)
+    iota(V("c4"), [[4, C]], 0)
+    iota(V("iow"), [[1, 256]], 0)
+    ms(V("half"), 0.5)
+    ms(V("z", 4 * A, 512), 0.0)
+    ms(V("a2"), 0.0)
+    ts(V("pi", 1, 2), V("pi", 0, 1), 15, Op.bitwise_and)
+    ts(V("pi", 2, 3), V("pi", 0, 1), 3, Op.bitwise_and)
+    ts(V("pi", 3, 4), V("pi", 0, 1), 2, Op.logical_shift_right, 3, Op.bitwise_and)
+    cp(V("ou"), V("oui"))
+    cp(V("pf", 0, 3), V("pi", 1, 4))
+    lcol, tcol, qcol, q1col, mulcol = [V("pf", i, i + 1) for i in range(5)]
+    ts(q1col, qcol, 1.0, Op.add)
+    ts(mulcol, qcol, 3.0, Op.is_equal, 2.0 ** -13, Op.max)
+    ts(V("mask"), V("m16"), lcol, Op.is_equal)
+    ts(V("nmask"), V("m16"), lcol, Op.not_equal)
+    ts(V("pa"), V("m4", 0, A), qcol, Op.not_equal)
+    ts(V("pb"), V("m4", 0, A), q1col, Op.is_equal, 8191.0, Op.mult)
+    for b in range(4):
+        o = V("et", 512 * b, 512 * b + 512)
+        add("g", lambda o=o, b=b: g.affine_select(o["ap"], T.half[:], [[1, 512]], Op.is_equal, 0.0, -b, -4), [V("half")], [o])
+    quant(V("qu"), V("su"), V("ut"))
+    add("v", lambda: g.vector.tensor_copy(T.qup[:].bitcast(dt.uint32), ind(V("qu"), V("ou"), True)["ap"]), [V("qu"), V("ou")], [V("qup")])
+    act(V("sup"), ind(V("su"), V("ou")), Fn.Copy)
+    act(V("cx"), V("l16"), Fn.Identity, bias=lcol)
+    act(V("cdo"), V("cx"), Fn.Identity, bias=float(WDO - WX))
+    act(V("c2"), V("cx"), Fn.Identity, bias=float(-C - 2 * WX), scale=2.0)
+    act(V("cval"), V("c4"), Fn.Identity, bias=tcol)
+
+    for t in range(R):
+        p = r ^ STEP[t]
+        qx, sx, lq, ls, eo, le, rk, lr = ["%s%d" % (n, t) for n in ("qx", "sx", "lq", "ls", "eo", "le", "rk", "lr")]
+        wdh = WAO + C if t else WDO
+        wah = wdh + A
+        wr4, wp4 = float(4 ** r), float(4 ** p)
+        quant(V(qx), V(sx), W(t, WX, WX + C))
+        mm("ps0", C, V("qup"), V("sup"), V(qx), V(sx))
+        mm("ps1", C, V("qup"), V("sup"), V(qx), V(sx))
+        if t:
+            send(p, V(lq, A, A + C), V(qx), "ao%d" % t, True)
+            send(p, V(ls, A, A + C), V(sx), "ao%d" % t)
+            arrive(p, [V(lq, A, A + C), V(ls, A, A + C)], "ao%d" % t)
+        else:
+            tt(V("pat"), V("pa"), V("pb"), Op.add)
+        if t == 2:
+            q = r ^ STEP[1]
+            o = q ^ STEP[0]
+            ts(L("rc"), L("zz"), 0.0, Op.is_gt)
+            ts(L("wr4"), L("wr"), wr4, Op.mult)
+            ts(L("wp4"), L("a"), float(4 ** q), Op.mult)
+            tt(digit(o), L("d%d" % o), L("rc"), Op.mult)
+        n1 = 16 * NV
+        for lo, hi in ((n1, C), (0, n1)):
+            tt(V("mm", lo, hi), V("ps0", lo, hi), V("mask", lo, hi), Op.mult)
+            if t == 2 and lo:
+                tt(L("dp"), L("d%d" % q), L("wp4"), Op.add)
+            if t == 2 and not lo:
+                tt(digit(q), L("dp"), L("rc"), Op.mult)
+            scan(V("hd", lo, hi), V("nmask", lo, hi), V("mm", lo, hi), 0.0, Op.mult, Op.add)
+            if t == 2 and lo:
+                tt(digit(r), digit(r), L("wr4"), Op.add)
+
+        def sc(k):
+            return V("hd", 16 * k + 15, 16 * k + 16)
+
+        def sign(k):
+            o = C * (k - NV)
+            act(V("sg", o, o + C), V("ps1", 0, C), Fn.Sign, bias=sc(k), scale=-1.0)
+
+        def count(k):
+            o, n = C * (k - NV), 16 * k + 16
+            act(V("sg", o, o + n), V("sg", o, o + n), Fn.Relu, acc=V("a1", k, k + 1))
+            if n < C:
+                act(V("sg", o + n, o + C), V("sg", o + n, o + C), Fn.Relu, scale=-1.0, acc=V("a2", k, k + 1))
+
+        sign(NV)
+        for k in range(NV, 20):
+            if k + 1 < 20: sign(k + 1)
+            count(k)
+
+        def compare(k):
+            o, n = C * k, 16 * k + 16
+            ts(V("fl", o, o + n), V("ps0", 0, n), sc(k), Op.is_ge)
+            ts(V("fl", o + n, o + C), V("ps0", n, C), sc(k), Op.is_gt)
+
+        def total(k):
+            o = C * k
+            scan(V("cum", 160 * k, 160 * k + 160), V("fl", o, o + 160), V("fl", o + 160, o + C), V("ini", k, k + 1), Op.add, Op.add)
+
+        tt(V("eq"), V("ps0", 0, C), V("hd"), Op.is_equal)
+        if t == 2:
+            cp(V("pre2"), V("gl", 160, 240))
+            send(p, V("lp2"), V("pre2"), "ap2")
+        compare(0)
+        scan(V("nc"), V("nmask"), V("eq"), 0.0, Op.mult, Op.subtract)
+        compare(1)
+        tt(V("ini"), V("nc", 15, C, 16), V("kc"), Op.add)
+        for k in range(NV):
+            if k + 2 < NV: compare(k + 2)
+            total(k)
+        ts(V(rk, 0, NV), V("cum", 159, 160 * NV, 160), 160.0, Op.add)
+        if t == 1:
+            o = p ^ STEP[0]
+            hi, lo = max(p, o), min(p, o)
+            arrive(p, [V("lp1")], "ap1")
+            ts(L("pw"), V("lp1"), 0.0, Op.is_gt)
+            ts(L("pm"), L("pk"), 0.0, Op.is_gt)
+            ts(L("d%d" % hi), V("lp1"), float(4 ** hi), Op.is_ge, float(4 ** hi), Op.mult)
+            cp(L("pkp"), V("lp1"))
+        lo = 0
+        for hi in CUTS:
+            a0 = max(lo, NV)
+            if hi > a0:
+                tt(V("a1", a0, hi), V("ini", a0, hi), V("a1", a0, hi), Op.subtract)
+                tt(V("a1", a0, hi), V("a1", a0, hi), V("a2", a0, hi), Op.add)
+                ts(V(rk, a0, hi), V("a1", a0, hi), 160.0, Op.add)
+            if hi == 20:
+                send(p, V(lr), V(rk), "ar%d" % t)
+                arrive(p, [V(lr)], "ar%d" % t)
+            cp(ind(V("e"), V(rk, lo, hi)), V("cval", 16 * lo, 16 * hi))
+            if lo == 0 and t == 1:
+                tt(L("d%d" % min(p, p ^ STEP[0])), L("pkp"), L("d%d" % max(p, p ^ STEP[0])), Op.subtract)
+            lo = hi
+        if t:
+            for b in range(4):
+                mm("ps%d" % (4 + b), C, E(b)[0], E(b)[1], V(lq, A, A + C), V(ls, A, A + C))
+            for b in range(3):
+                act(W(t, WDO, WAO, b), V("ps%d" % (4 + b), 0, C), Fn.Copy, scale=2.0)
+        scan(V("es"), V("pat"), V("e", 0, A), 0.0, Op.mult, Op.add)
+        cp(L("rk"), V(rk))
+        ts(V(eo), V("es", 3, A, 4), mulcol, Op.mult)
+        ts(L("u"), V(rk), float(A), Op.is_ge, BIG, Op.mult)
+        cp(V("z", 0, 192), ind(W(t, WX, WX + C), V(eo, 0, 12)))
+        act(V("z", 192, 384), ind(W(t, WX, WX + C), V(eo, 12, 24)), Fn.Copy)
+        send(p, V(le), V(eo), "ae%d" % t)
+        arrive(p, [V(le)], "ae%d" % t)
+        tt(L("v"), L("rk"), L("u"), Op.add)
+        quant(V("qz"), V("sz"), V("z"))
+        for b in range(4):
+            mm("ps%d" % b, 128, V("qw", 128 * b, 128 * b + 128), V("sw", 128 * b, 128 * b + 128), V("qz"), V("sz"))
+        if t:
+            act(W(t, WDO, WAO, 3), V("ps7", 0, C), Fn.Copy, scale=2.0)
+        tt(L("smid"), L("v"), V("cx"), Op.min)
+        ts(L("wr"), V(rk), float(A), Op.is_lt)
+
+        def moffs(lo, hi):
+            for b in range(lo, hi):
+                ts(V("moff", 20 * b, 20 * b + 20), L("smid"), 4.0, Op.mult, float(b), Op.add)
+
+        moffs(0, 2)
+        for b in range(4):
+            act(V("rl", A * b, A * b + A), V("ps%d" % b, 0, A), Fn.Relu, scale=0.03125)
+            tt(W(t, WH, WX, b), V("rl", A * b, A * b + A), V("z", b, 4 * A, 4), Op.add)
+        quant(V("qh%d" % t), V("sh%d" % t), W(t, 0, 128))
+        send(p, V(lq, 0, A), V("qh%d" % t, 0, A), "ah%d" % t, True)
+        send(p, V(ls, 0, A), V("sh%d" % t, 0, A), "ah%d" % t)
+        arrive(p, [V(lq, 0, A), V(ls, 0, A)], "ah%d" % t)
+        if t == 2:
+            arrive(p, [V("lp2")], "ap2")
+            cp(V("pd"), V("lp2"))
+        moffs(2, 3)
+        if t == 2:
+            tt(V("dd"), V("pd"), V("gl", 160, 240), Op.subtract)
+        moffs(3, 4)
+
+        def halve(b):
+            act(V("xh", b, 4 * C, 4), ind(W(t, 0, WX + C), V("moff", 20 * b, 20 * b + 20)), Fn.Copy, scale=0.5)
+
+        def mean(b):
+            tt(W(t, WAO, WAO + C, b), V("xh", b, 4 * C, 4), V("ps%d" % (4 + b), 0, C), Op.add)
+
+        def foffs():
+            tt(L("fin"), L("zz"), L("smid"), Op.max)
+            for b in range(4):
+                ts(V("foff", 20 * b, 20 * b + 20), L("fin"), 4.0, Op.mult, float(b), Op.add)
+
+        if t == 0:
+            for b in range(4):
+                halve(b)
+            quant(V("qe"), V("se"), V("et"))
+            quant(V(lq, A, A + 128), V(ls, A, A + 128), W(0, WX, WX + 128))
+            ts(L("m96"), L("wr"), float(A), Op.mult)
+            ts(L("vpf"), V(lr), float(wdh), Op.add)
+            ts(L("a"), V(lr), float(A), Op.is_lt)
+            tt(L("sh"), L("vpf"), L("m96"), Op.add)
+            ts(digit(r), L("wr"), wr4, Op.mult)
+            tt(L("zz"), L("sh"), L("a"), Op.mult)
+            ts(digit(p), L("a"), wp4, Op.mult)
+            foffs()
+            tt(L("pk"), digit(r), digit(p), Op.add)
+            ts(V("rs"), V("m4"), 0.0, Op.not_equal)
+            cp(V("pre1"), L("pk"))
+            send(r ^ STEP[1], V("lp1"), V("pre1"), "ap1")
+            quant(V("qv"), V("sv"), V("vt"))
+        else:
+            halve(0); halve(1)
+            if t == 2:
+                ts(V("gl", 0, 80), V("dd"), 0.0, Op.max)
+                ts(V("gl", 80, 160), V("dd"), 0.0, Op.min)
+            ts(L("a"), V(lr), float(A), Op.is_lt)
+            if t == 2:
+                scan(V("gs"), V("rs"), V("gl"), 0.0, Op.mult, Op.add)
+            ts(L("vpf"), V(lr), float(wdh), Op.add)
+            if t == 2:
+                ts(L("pw"), V("gs", 3, 80, 4), 0.0, Op.is_gt)
+                ts(L("pm"), V("gs", 83, 160, 4), 0.0, Op.is_lt)
+            tt(L("wv"), L("a"), L("pw"), Op.max)
+            tt(L("m"), L("wr"), L("pm"), Op.max)
+            cp(V("wu"), L("wv"))
+            act(V("wrow"), ind(V("iow"), V("wu")), Fn.Copy)
+            ts(L("m96"), L("m"), float(A), Op.mult)
+            ts(L("m320"), L("m"), float(C), Op.mult)
+            mean(0)
+            tt(L("sh"), L("vpf"), L("m96"), Op.add)
+            tt(L("so"), L("m320"), V("cdo"), Op.add)
+            mean(1)
+            scan(V("wcum"), V("wrow"), V("wrow"), 0.0, Op.add, Op.max)
+            halve(2)
+            act(V("junk"), V("wcum"), Fn.Sign, bias=K + 0.5, scale=-1.0, acc=V("acc", 0, 1))
+            halve(3)
+            tt(L("sha"), L("sh"), L("a"), Op.mult)
+            tt(L("sel"), L("sha"), L("so"), Op.max)
+            mean(2)
+            tt(L("sel2"), L("sel"), L("wv"), Op.mult)
+            ts(L("cut"), V("c2"), V("acc", 0, 1), Op.is_lt)
+            tt(L("zz"), L("sel2"), L("cut"), Op.mult)
+            foffs()
+            mean(3)
+        act(V("own"), ind(V("xh"), V(le)), Fn.Copy)
+        for b in range(4):
+            mm("ps%d" % b, 128, E(b)[0], E(b)[1], V(lq, 0, 128), V(ls, 0, 128))
+        for b in range(4):
+            act(W(t, wdh, wah, b), V("ps%d" % b, 0, A), Fn.Copy, scale=2.0)
+            tt(W(t, wah, wah + A, b), V("own", b, 4 * A, 4), V("ps%d" % b, 0, A), Op.add)
+        whole = W(t, 0, wah + A)
+        for b in range(2):
+            cp(W(t + 1, WX, WX + C, b), ind(whole, V("foff", 20 * b, 20 * b + 20)))
+            act(W(t + 1, WX, WX + C, b + 2), ind(whole, V("foff", 20 * b + 40, 20 * b + 60)), Fn.Copy)
+
+    quant(V("qx3"), V("sx3"), W(R, WX, WX + C))
+    mm("ps0", C, V("qv"), V("sv"), V("qx3"), V("sx3"))
+    store("y", T.oc[:], V("qx3"), T.qx3[:].bitcast(dt.uint8))
+    for k in range(4):
+        store("ys"[k % 2], T.osc[4 * k:4 * k + 4, :], V("sx3"), T.sx3[32 * k:32 * k + 4, :])
+    act(V("yo"), V("ps0", 0, C), Fn.Copy)
+    store("s", T.y[:], V("yo"), T.yo[:])
+    ts(L("wp4"), L("a"), wp4, Op.mult)
+    ts(L("wr4"), L("wr"), wr4, Op.mult)
+    ts(L("rc"), L("zz"), 0.0, Op.is_gt)
+    tt(L("dp"), L("wp4"), V("gs", 3, 80, 4), Op.add)
+    tt(L("pk"), L("wr4"), V("gs", 163, 240, 4), Op.add)
+    tt(L("pkp"), L("dp"), L("rc"), Op.mult)
+    tt(L("ov"), L("pkp"), L("pk"), Op.add)
+    cp(V("ovu"), L("ov"))
+    cp(V("ovr"), ind(V("iow"), V("ovu")))
+    store("y", T.ov[:], V("ovr"), T.ovr[0:128:16, :])
+
+    known = {q: {} for q in queues}
+    for o in ops:
+        if o["q"] is None:
+            o["clock"] = {}
+            continue
+        kn = known[o["q"]]
+        for d in sorted(o["deps"], reverse=True):
+            e = ops[d]
+            if kn.get(e["stream"], -1) >= e["seq"]:
+                continue
+            e["need"] = True
+            o["waits"].append(e)
+            kn[e["stream"]] = e["seq"]
+            for s, n in e["clock"].items():
+                kn[s] = max(kn.get(s, -1), n)
+        o["clock"] = dict(kn)
+    n = {q: 0 for q in queues}
+    for o in ops:
+        if o["q"] is None:
+            continue
+        for e in o["waits"]:
+            queues[o["q"]].wait_ge(T.sem[e["token"][0]], e["token"][1])
+        ins = o["fn"]()
+        if o["token"] is None and o["need"]:
+            n[o["q"]] += 1
+            o["token"] = ("c" + o["q"], n[o["q"]])
+            ins.then_inc(T.sem[o["token"][0]], 1)
+    g.wait_ge(T.sem.sent, sent[0])
+    g.wait_ge(T.sem.out, stored[0])

@@ -4,9 +4,15 @@ from concourse.mybir import dt, AluOpType as Op, ActivationFunctionType as Fn
 C, A, K, R = 320, 96, 128, 3
 STEP = [1, 2, 3]
 NV = 11
-CUTS = [10, 20]
-WH, WX, WDO, WAO, WEND = 0, 96, 416, 736, 1248
+SP = 10
+MID = 18
+FIRST = "ps0"
+HV = 0
+DV = 1
+WH, WX, WDO, WDH, WAO, WEND = 0, 96, 416, 736, 832, 1248
 BIG = 4096.0
+OFF = 1024.0
+UNIT = 2048.0
 
 F, B, U, I, Q, S = "float32", "bfloat16", "uint16", "int32", "float8_e4m3fn_x4", "uint8"
 SCRATCH = {}
@@ -23,7 +29,9 @@ for _t in range(R):
     _buf("lq%d" % _t, A + C, Q); _buf("ls%d" % _t, A + C, S)
     _buf("eo%d" % _t, 24, U); _buf("le%d" % _t, 24, U); _buf("rk%d" % _t, 20, U); _buf("lr%d" % _t, 20, U)
 _buf("win3", 4 * (WX + C), B); _buf("qx3", C, Q); _buf("sx3", C, S)
-_buf("pre1", 20, U); _buf("lp1", 20, U); _buf("pre2", 80, U); _buf("lp2", 80, U)
+_buf("pre1", 20, B); _buf("lp1", 20, B); _buf("lp2", 80, B)
+for _t in (1, 2):
+    _buf("acc%d" % _t, 1, F); _buf("la%d" % _t, 1, F)
 for _n in "uv":
     _buf(_n + "t", 512, B); _buf("q" + _n, 128, Q); _buf("s" + _n, 128, S)
 _buf("qup", 128, Q); _buf("sup", 128, S)
@@ -36,15 +44,16 @@ for _b in range(8):
 _buf("pi", 4, I); _buf("pf", 8, F); _buf("oui", 8, I); _buf("ou", 8, U)
 _buf("m16", C, F); _buf("mask", C, B); _buf("nmask", C, B); _buf("kc", 20, F)
 _buf("c4", C, F); _buf("cval", C, F); _buf("l16", 20, F); _buf("cx", 20, F); _buf("cdo", 20, F); _buf("c2", 20, F)
-_buf("m4", 240, F); _buf("pa", A, F); _buf("pb", A, F); _buf("pat", A, F); _buf("rs", 240, F); _buf("iow", 256, B)
-_buf("mm", C, F); _buf("hd", C, F); _buf("eq", C, B); _buf("nc", C, B); _buf("ini", 20, B)
+_buf("m4", 240, F); _buf("pa", A, F); _buf("pb", A, F); _buf("pat", A, F); _buf("rs", 240, B); _buf("iow", 256, B)
+_buf("mm", C, F); _buf("hd", C, F); _buf("eq", C, B); _buf("nc", C, B); _buf("ini", 20, F)
 _buf("fl", NV * C, B); _buf("cum", NV * 160, B); _buf("sg", (20 - NV) * C, B); _buf("junk", C, B)
-_buf("a1", 20, F); _buf("a2", 20, F); _buf("e", C, F); _buf("es", A, F)
-_buf("moff", 80, U); _buf("foff", 80, U); _buf("wu", 20, U); _buf("wrow", C, B); _buf("wcum", C, B); _buf("acc", 2, F)
-_buf("sm", 40 * 20, F)
-_buf("pd", 80, F); _buf("dd", 80, F); _buf("gl", 240, F); _buf("gs", 240, F); _buf("ovu", 20, U); _buf("ovr", C, F)
+_buf("sq", 80, F); _buf("so", 80, F); _buf("e", C, F); _buf("es", A, F)
+_buf("moff", 80, U); _buf("foff", 80, U); _buf("wu", 20, U); _buf("wrow", C, B); _buf("wcum", C, B)
+_buf("fa", 80, F); _buf("fb", 80, F); _buf("fo", 80, F)
+_buf("sm", 24 * 20, F)
+_buf("dd", 80, B); _buf("gl", 240, B); _buf("gs", 240, B); _buf("ovu", 20, U); _buf("ovr", C, F)
 
-SEMAPHORES = ["cv", "cs", "ct", "cg", "lx", "lu", "lw", "lws", "lv", "out", "sent", "ap1", "ap2", "ao1", "ao2"] + \
+SEMAPHORES = ["cv", "cs", "ct", "cg", "lx", "lu", "lw", "lws", "lv", "out", "sent", "ap1", "ap2", "ao1", "ao2", "ac1", "ac2"] + \
     ["%s%d" % (n, t) for t in range(R) for n in ("ae", "ar", "ah")]
 
 
@@ -111,6 +120,12 @@ def rank_program(g, core, T, topo):
         if acc is not None: kw["accum_out"] = ap(acc)
         add("s", lambda: g.scalar.activation(ap(o), ap(a), fn, **kw), [a, bias, scale], [o] + ([acc] if acc else []))
 
+    def scaled(vector, o, a, c):
+        if vector:
+            ts(o, a, c, Op.mult)
+        else:
+            act(o, a, Fn.Copy, scale=c)
+
     def mm(o, n, lq, ls, rq, rs):
         add("t", lambda: g.tensor.matmul_mx(T[o][:, 0:n], ap(lq), ap(ls), ap(rq), ap(rs), True, True), [lq, ls, rq, rs], [V(o)])
 
@@ -150,8 +165,14 @@ def rank_program(g, core, T, topo):
     def digit(i):
         return V("gl", 160 + i, 240, 4)
 
+    def four(name, i):
+        return V(name, i, 80, 4)
+
     def E(b):
         return V("qe", 128 * b, 128 * b + 128), V("se", 128 * b, 128 * b + 128)
+
+    n1 = 16 * SP
+    upper, lower = (n1, C), (0, n1)
 
     load("y", W(0, WX, WX + C), W(0, WX, WX + C)["ap"], T.x[:], "lx")
     load("s", V("ut"), T.ut[:], T.u[:], "lu")
@@ -162,18 +183,21 @@ def rank_program(g, core, T, topo):
     iota(V("oui"), [[16, 8]], 0, 0, False)
     iota(V("m16"), [[0, 20], [1, 16]], 0)
     iota(V("m4"), [[0, 60], [1, 4]], 0)
-    iota(V("kc", 0, NV), [[0, NV]], -160)
-    iota(V("kc", NV, 20), [[16, 20 - NV]], 16 * NV + 16 - 160)
-    iota(V("l16"), [[16, 20]], WX)
+    iota(V("kc"), [[16, 20]], 16)
+    iota(V("l16"), [[16, 20]], WX + int(OFF))
     iota(V("c4"), [[4, C]], 0)
     iota(V("iow"), [[1, 256]], 0)
     ms(V("half"), 0.5)
     ms(V("z", 4 * A, 512), 0.0)
-    ms(V("a2"), 0.0)
+    ms(V("sq"), 0.0)
+    ms(V("fa"), 0.0)
+    ms(V("fb"), 0.0)
     ts(V("pi", 1, 2), V("pi", 0, 1), 15, Op.bitwise_and)
     ts(V("pi", 2, 3), V("pi", 0, 1), 3, Op.bitwise_and)
     ts(V("pi", 3, 4), V("pi", 0, 1), 2, Op.logical_shift_right, 3, Op.bitwise_and)
     cp(V("ou"), V("oui"))
+    ms(four("fa", 0), -4 * BIG)
+    ms(four("fb", 2), -4 * BIG)
     cp(V("pf", 0, 3), V("pi", 1, 4))
     lcol, tcol, qcol, q1col, mulcol = [V("pf", i, i + 1) for i in range(5)]
     ts(q1col, qcol, 1.0, Op.add)
@@ -182,6 +206,7 @@ def rank_program(g, core, T, topo):
     ts(V("nmask"), V("m16"), lcol, Op.not_equal)
     ts(V("pa"), V("m4", 0, A), qcol, Op.not_equal)
     ts(V("pb"), V("m4", 0, A), q1col, Op.is_equal, 8191.0, Op.mult)
+    ts(V("rs"), V("m4"), 0.0, Op.not_equal)
     for b in range(4):
         o = V("et", 512 * b, 512 * b + 512)
         add("g", lambda o=o, b=b: g.affine_select(o["ap"], T.half[:], [[1, 512]], Op.is_equal, 0.0, -b, -4), [V("half")], [o])
@@ -190,41 +215,37 @@ def rank_program(g, core, T, topo):
     act(V("sup"), ind(V("su"), V("ou")), Fn.Copy)
     act(V("cx"), V("l16"), Fn.Identity, bias=lcol)
     act(V("cdo"), V("cx"), Fn.Identity, bias=float(WDO - WX))
-    act(V("c2"), V("cx"), Fn.Identity, bias=float(-C - 2 * WX), scale=2.0)
+    act(V("c2"), V("cx"), Fn.Identity, bias=float(-C - 2 * WX - 2 * OFF), scale=2.0)
     act(V("cval"), V("c4"), Fn.Identity, bias=tcol)
+
+    def gather(t, piece):
+        lo, hi = piece
+        whole = W(t - 1, 0, WEND if t > 1 else WDO + 2 * A)
+        for b in range(4):
+            o, a = W(t, WX + lo, WX + hi, b), ind(whole, V("foff", 20 * b + lo // 16, 20 * b + hi // 16))
+            if b < 2:
+                cp(o, a)
+            else:
+                act(o, a, Fn.Copy)
+
+    def pack(t, piece):
+        lo, hi = piece
+        quant(V("qx%d" % t, lo, hi), V("sx%d" % t, lo, hi), W(t, WX + lo, WX + hi))
 
     for t in range(R):
         p = r ^ STEP[t]
         qx, sx, lq, ls, eo, le, rk, lr = ["%s%d" % (n, t) for n in ("qx", "sx", "lq", "ls", "eo", "le", "rk", "lr")]
-        wdh = WAO + C if t else WDO
-        wah = wdh + A
-        wr4, wp4 = float(4 ** r), float(4 ** p)
-        quant(V(qx), V(sx), W(t, WX, WX + C))
-        mm("ps0", C, V("qup"), V("sup"), V(qx), V(sx))
-        mm("ps1", C, V("qup"), V("sup"), V(qx), V(sx))
-        if t:
-            send(p, V(lq, A, A + C), V(qx), "ao%d" % t, True)
-            send(p, V(ls, A, A + C), V(sx), "ao%d" % t)
-            arrive(p, [V(lq, A, A + C), V(ls, A, A + C)], "ao%d" % t)
-        else:
-            tt(V("pat"), V("pa"), V("pb"), Op.add)
-        if t == 2:
-            q = r ^ STEP[1]
-            o = q ^ STEP[0]
-            ts(L("rc"), L("zz"), 0.0, Op.is_gt)
-            ts(L("wr4"), L("wr"), wr4, Op.mult)
-            ts(L("wp4"), L("a"), float(4 ** q), Op.mult)
-            tt(digit(o), L("d%d" % o), L("rc"), Op.mult)
-        n1 = 16 * NV
-        for lo, hi in ((n1, C), (0, n1)):
-            tt(V("mm", lo, hi), V("ps0", lo, hi), V("mask", lo, hi), Op.mult)
-            if t == 2 and lo:
-                tt(L("dp"), L("d%d" % q), L("wp4"), Op.add)
-            if t == 2 and not lo:
-                tt(digit(q), L("dp"), L("rc"), Op.mult)
-            scan(V("hd", lo, hi), V("nmask", lo, hi), V("mm", lo, hi), 0.0, Op.mult, Op.add)
-            if t == 2 and lo:
-                tt(digit(r), digit(r), L("wr4"), Op.add)
+        wdh, gap = (WDH, WAO - WDO) if t else (WDO, A)
+        wr4, wp4 = UNIT * 4 ** r, UNIT * 4 ** p
+        scores = {upper: V("ps2", 0, C - n1), lower: V("ps0", 0, n1)}
+
+        def masked(piece): tt(V("mm", *piece), scores[piece], V("mask", *piece), Op.mult)
+        def hold(piece): scan(V("hd", *piece), V("nmask", *piece), V("mm", *piece), 0.0, Op.mult, Op.add)
+        def equal(piece): tt(V("eq", *piece), scores[piece], V("hd", *piece), Op.is_equal)
+        def ties(piece): scan(V("nc", *piece), V("nmask", *piece), V("eq", *piece), 0.0, Op.mult, Op.subtract)
+
+        def tie(lo, hi):
+            return V("nc", 16 * lo + 15, 16 * hi, 16)
 
         def sc(k):
             return V("hd", 16 * k + 15, 16 * k + 16)
@@ -235,14 +256,10 @@ def rank_program(g, core, T, topo):
 
         def count(k):
             o, n = C * (k - NV), 16 * k + 16
-            act(V("sg", o, o + n), V("sg", o, o + n), Fn.Relu, acc=V("a1", k, k + 1))
+            fn, b = (Fn.Sign, 0.5) if k < MID else (Fn.Relu, 0.0)
+            act(V("sg", o, o + n), V("sg", o, o + n), fn, bias=b, scale=-1.0 if b else 1.0, acc=V("sq", 4 * k + 1, 4 * k + 2))
             if n < C:
-                act(V("sg", o + n, o + C), V("sg", o + n, o + C), Fn.Relu, scale=-1.0, acc=V("a2", k, k + 1))
-
-        sign(NV)
-        for k in range(NV, 20):
-            if k + 1 < 20: sign(k + 1)
-            count(k)
+                act(V("sg", o + n, o + C), V("sg", o + n, o + C), fn, bias=-b, scale=-1.0, acc=V("sq", 4 * k + 2, 4 * k + 3))
 
         def compare(k):
             o, n = C * k, 16 * k + 16
@@ -253,171 +270,194 @@ def rank_program(g, core, T, topo):
             o = C * k
             scan(V("cum", 160 * k, 160 * k + 160), V("fl", o, o + 160), V("fl", o + 160, o + C), V("ini", k, k + 1), Op.add, Op.add)
 
-        tt(V("eq"), V("ps0", 0, C), V("hd"), Op.is_equal)
-        if t == 2:
-            cp(V("pre2"), V("gl", 160, 240))
-            send(p, V("lp2"), V("pre2"), "ap2")
-        compare(0)
-        scan(V("nc"), V("nmask"), V("eq"), 0.0, Op.mult, Op.subtract)
-        compare(1)
-        tt(V("ini"), V("nc", 15, C, 16), V("kc"), Op.add)
-        for k in range(NV):
-            if k + 2 < NV: compare(k + 2)
-            total(k)
-        ts(V(rk, 0, NV), V("cum", 159, 160 * NV, 160), 160.0, Op.add)
-        if t == 1:
-            o = p ^ STEP[0]
-            hi, lo = max(p, o), min(p, o)
-            arrive(p, [V("lp1")], "ap1")
-            ts(L("pw"), V("lp1"), 0.0, Op.is_gt)
-            ts(L("pm"), L("pk"), 0.0, Op.is_gt)
-            ts(L("d%d" % hi), V("lp1"), float(4 ** hi), Op.is_ge, float(4 ** hi), Op.mult)
-            cp(L("pkp"), V("lp1"))
-        lo = 0
-        for hi in CUTS:
-            a0 = max(lo, NV)
-            if hi > a0:
-                tt(V("a1", a0, hi), V("ini", a0, hi), V("a1", a0, hi), Op.subtract)
-                tt(V("a1", a0, hi), V("a1", a0, hi), V("a2", a0, hi), Op.add)
-                ts(V(rk, a0, hi), V("a1", a0, hi), 160.0, Op.add)
-            if hi == 20:
-                send(p, V(lr), V(rk), "ar%d" % t)
-                arrive(p, [V(lr)], "ar%d" % t)
+        def invert(lo, hi):
             cp(ind(V("e"), V(rk, lo, hi)), V("cval", 16 * lo, 16 * hi))
-            if lo == 0 and t == 1:
-                tt(L("d%d" % min(p, p ^ STEP[0])), L("pkp"), L("d%d" % max(p, p ^ STEP[0])), Op.subtract)
-            lo = hi
+
+        def dold(b, vector=False):
+            if t:
+                scaled(vector, W(t, WDO, WDH, b), V("ps%d" % (4 + b), 0, C), 2.0)
+
+        if t: gather(t, upper)
+        pack(t, upper)
+        mm("ps2", C - n1, V("qup"), V("sup"), V(qx, n1, C), V(sx, n1, C))
+        if t:
+            gather(t, lower)
+            masked(upper)
+        pack(t, lower)
+        for bank in sorted(("ps0", "ps1"), key=lambda b: b != FIRST):
+            mm(bank, C, V("qup"), V("sup"), V(qx), V(sx))
+        if t:
+            send(p, V(lq, A, A + C), V(qx), "ao%d" % t, True)
+            send(p, V(ls, A, A + C), V(sx), "ao%d" % t)
+            arrive(p, [V(lq, A, A + C), V(ls, A, A + C)], "ao%d" % t)
+        else:
+            masked(upper)
+            tt(V("pat"), V("pa"), V("pb"), Op.add)
+        hold(upper)
+        if t == 1:
+            ts(L("nb"), V("pre1"), 1.0, Op.is_lt, BIG, Op.mult)
+        equal(upper)
+        sign(NV)
+        for k in range(NV, 20):
+            if k + 1 < 20: sign(k + 1)
+            count(k)
+        rows = list(range(SP, NV)) + list(range(SP))
+        masked(lower)
+        for k in rows[:NV - SP]: compare(k)
+        hold(lower)
+        ties(upper)
+        ts(V("sq", 4 * NV, 4 * MID, 4), tie(NV, MID), 2.0, Op.mult)
+        tt(V("ini", MID, 20), tie(MID, 20), V("kc", MID, 20), Op.add)
+        compare(0)
+        equal(lower)
+        compare(1)
+        ties(lower)
+        compare(2)
+        ts(V("ini", 0, NV), tie(0, NV), -160.0, Op.add)
+        for i, k in enumerate(rows):
+            if k + 3 + NV - SP < SP + NV - SP and k < SP: compare(k + 3)
+            total(k)
+        scan(V("so", 4 * NV, 4 * MID), V("rs", 4 * NV, 4 * MID), V("sq", 4 * NV, 4 * MID), 0.0, Op.mult, Op.add)
+        if t == 2:
+            arrive(p, [V("lp2")], "ap2")
+            tt(V("dd"), V("lp2"), V("gl", 160, 240), Op.subtract)
+        ts(V(rk, 0, NV), V("cum", 159, 160 * NV, 160), 160.0, Op.add)
+        ts(V(rk, NV, MID), V("so", 4 * NV + 2, 4 * MID, 4), 0.5, Op.mult, 160.0, Op.add)
+        if t == 2:
+            ts(V("gl", 0, 80), V("dd"), 0.0, Op.max)
+            ts(V("gl", 80, 160), V("dd"), -1.0, Op.mult, 0.0, Op.max)
+        invert(0, MID)
+        for k in range(MID, 20):
+            ts(V(rk, k, k + 1), V("sq", 4 * k + 2, 4 * k + 3), V("sq", 4 * k + 1, 4 * k + 2), Op.subtract, V("ini", k, k + 1), Op.add)
+        send(p, V(lr), V(rk), "ar%d" % t)
+        arrive(p, [V(lr)], "ar%d" % t)
+        if t == 2:
+            scan(V("gs"), V("rs"), V("gl"), 0.0, Op.mult, Op.add)
+        invert(MID, 20)
         if t:
             for b in range(4):
                 mm("ps%d" % (4 + b), C, E(b)[0], E(b)[1], V(lq, A, A + C), V(ls, A, A + C))
-            for b in range(3):
-                act(W(t, WDO, WAO, b), V("ps%d" % (4 + b), 0, C), Fn.Copy, scale=2.0)
-        scan(V("es"), V("pat"), V("e", 0, A), 0.0, Op.mult, Op.add)
-        cp(L("rk"), V(rk))
-        ts(V(eo), V("es", 3, A, 4), mulcol, Op.mult)
+        dold(0); dold(1)
         ts(L("u"), V(rk), float(A), Op.is_ge, BIG, Op.mult)
+        if t == 2:
+            ts(L("nb"), V("gs", 83, 160, 4), 1.0, Op.is_lt, BIG, Op.mult)
+        scan(V("es"), V("pat"), V("e", 0, A), 0.0, Op.mult, Op.add)
+        nw = L("nw") if t else L("u")
+        if t:
+            tt(nw, L("u"), L("nb"), Op.min)
+        ts(L("rk"), V(rk), OFF, Op.add)
+        ts(V(eo), V("es", 3, A, 4), mulcol, Op.mult)
+        if t:
+            ts(V("wu"), nw, 1.0, Op.is_lt)
+        tt(L("v"), L("rk"), L("u"), Op.add)
         cp(V("z", 0, 192), ind(W(t, WX, WX + C), V(eo, 0, 12)))
         act(V("z", 192, 384), ind(W(t, WX, WX + C), V(eo, 12, 24)), Fn.Copy)
         send(p, V(le), V(eo), "ae%d" % t)
         arrive(p, [V(le)], "ae%d" % t)
-        tt(L("v"), L("rk"), L("u"), Op.add)
+        tt(four("fb", 3), L("v"), V("cx"), Op.min)
         quant(V("qz"), V("sz"), V("z"))
         for b in range(4):
             mm("ps%d" % b, 128, V("qw", 128 * b, 128 * b + 128), V("sw", 128 * b, 128 * b + 128), V("qz"), V("sz"))
         if t:
-            act(W(t, WDO, WAO, 3), V("ps7", 0, C), Fn.Copy, scale=2.0)
-        tt(L("smid"), L("v"), V("cx"), Op.min)
-        ts(L("wr"), V(rk), float(A), Op.is_lt)
-
-        def moffs(lo, hi):
-            for b in range(lo, hi):
-                ts(V("moff", 20 * b, 20 * b + 20), L("smid"), 4.0, Op.mult, float(b), Op.add)
-
-        moffs(0, 2)
+            act(V("wrow"), ind(V("iow"), V("wu")), Fn.Copy)
+        for b in range(4):
+            ts(V("moff", 20 * b, 20 * b + 20), four("fb", 3), 4.0, Op.mult, b - 4 * OFF, Op.add)
+        ts(four("fa", 2), nw, 1.0, Op.is_lt, float(gap), Op.mult)
+        if t:
+            scan(V("wcum"), V("wrow"), V("wrow"), 0.0, Op.add, Op.max)
         for b in range(4):
             act(V("rl", A * b, A * b + A), V("ps%d" % b, 0, A), Fn.Relu, scale=0.03125)
             tt(W(t, WH, WX, b), V("rl", A * b, A * b + A), V("z", b, 4 * A, 4), Op.add)
+        if t:
+            act(V("junk"), V("wcum"), Fn.Sign, bias=K + 0.5, scale=-1.0, acc=V("acc%d" % t))
+            send(p, V("la%d" % t), V("acc%d" % t), "ac%d" % t)
+            arrive(p, [V("la%d" % t)], "ac%d" % t)
+        dold(2)
         quant(V("qh%d" % t), V("sh%d" % t), W(t, 0, 128))
         send(p, V(lq, 0, A), V("qh%d" % t, 0, A), "ah%d" % t, True)
         send(p, V(ls, 0, A), V("sh%d" % t, 0, A), "ah%d" % t)
         arrive(p, [V(lq, 0, A), V(ls, 0, A)], "ah%d" % t)
-        if t == 2:
-            arrive(p, [V("lp2")], "ap2")
-            cp(V("pd"), V("lp2"))
-        moffs(2, 3)
-        if t == 2:
-            tt(V("dd"), V("pd"), V("gl", 160, 240), Op.subtract)
-        moffs(3, 4)
 
         def halve(b):
-            act(V("xh", b, 4 * C, 4), ind(W(t, 0, WX + C), V("moff", 20 * b, 20 * b + 20)), Fn.Copy, scale=0.5)
+            scaled(b < HV, V("xh", b, 4 * C, 4), ind(W(t, 0, WX + C), V("moff", 20 * b, 20 * b + 20)), 0.5)
 
         def mean(b):
             tt(W(t, WAO, WAO + C, b), V("xh", b, 4 * C, 4), V("ps%d" % (4 + b), 0, C), Op.add)
 
-        def foffs():
-            tt(L("fin"), L("zz"), L("smid"), Op.max)
-            for b in range(4):
-                ts(V("foff", 20 * b, 20 * b + 20), L("fin"), 4.0, Op.mult, float(b), Op.add)
+        def sources():
+            scan(V("fo"), V("fa"), V("fb"), 0.0, Op.add, Op.max)
 
-        if t == 0:
+        def foffs():
             for b in range(4):
-                halve(b)
+                ts(V("foff", 20 * b, 20 * b + 20), four("fo", 3), 4.0, Op.mult, b - 4 * OFF, Op.add)
+
+        for b in range(4):
+            halve(b)
+        dold(3, DV)
+        ts(four("fa", 1), V(lr), wdh + OFF, Op.add)
+        ts(four("fb", 0), V(lr), float(A), Op.is_ge, -BIG, Op.mult)
+        if t == 0:
+            ts(digit(p), V(lr), float(A), Op.is_lt, wp4, Op.mult)
+            ts(digit(r), V(rk), float(A), Op.is_lt, wr4, Op.mult)
+            sources()
+            tt(V("pre1"), digit(r), digit(p), Op.add)
+            foffs()
+            send(r ^ STEP[1], V("lp1"), V("pre1"), "ap1")
             quant(V("qe"), V("se"), V("et"))
             quant(V(lq, A, A + 128), V(ls, A, A + 128), W(0, WX, WX + 128))
-            ts(L("m96"), L("wr"), float(A), Op.mult)
-            ts(L("vpf"), V(lr), float(wdh), Op.add)
-            ts(L("a"), V(lr), float(A), Op.is_lt)
-            tt(L("sh"), L("vpf"), L("m96"), Op.add)
-            ts(digit(r), L("wr"), wr4, Op.mult)
-            tt(L("zz"), L("sh"), L("a"), Op.mult)
-            ts(digit(p), L("a"), wp4, Op.mult)
-            foffs()
-            tt(L("pk"), digit(r), digit(p), Op.add)
-            ts(V("rs"), V("m4"), 0.0, Op.not_equal)
-            cp(V("pre1"), L("pk"))
-            send(r ^ STEP[1], V("lp1"), V("pre1"), "ap1")
             quant(V("qv"), V("sv"), V("vt"))
         else:
-            halve(0); halve(1)
-            if t == 2:
-                ts(V("gl", 0, 80), V("dd"), 0.0, Op.max)
-                ts(V("gl", 80, 160), V("dd"), 0.0, Op.min)
-            ts(L("a"), V(lr), float(A), Op.is_lt)
-            if t == 2:
-                scan(V("gs"), V("rs"), V("gl"), 0.0, Op.mult, Op.add)
-            ts(L("vpf"), V(lr), float(wdh), Op.add)
-            if t == 2:
-                ts(L("pw"), V("gs", 3, 80, 4), 0.0, Op.is_gt)
-                ts(L("pm"), V("gs", 83, 160, 4), 0.0, Op.is_lt)
-            tt(L("wv"), L("a"), L("pw"), Op.max)
-            tt(L("m"), L("wr"), L("pm"), Op.max)
-            cp(V("wu"), L("wv"))
-            act(V("wrow"), ind(V("iow"), V("wu")), Fn.Copy)
-            ts(L("m96"), L("m"), float(A), Op.mult)
-            ts(L("m320"), L("m"), float(C), Op.mult)
+            if t == 1:
+                arrive(p, [V("lp1")], "ap1")
+            ahead = V("lp1") if t == 1 else V("gs", 3, 80, 4)
+            tt(four("fb", 1), V("cdo"), ahead, Op.min)
+            ts(L("wp4"), V(lr), float(A), Op.is_lt, wp4, Op.mult)
+            ts(L("wr4"), V(rk), float(A), Op.is_lt, wr4, Op.mult)
             mean(0)
-            tt(L("sh"), L("vpf"), L("m96"), Op.add)
-            tt(L("so"), L("m320"), V("cdo"), Op.add)
-            mean(1)
-            scan(V("wcum"), V("wrow"), V("wrow"), 0.0, Op.add, Op.max)
-            halve(2)
-            act(V("junk"), V("wcum"), Fn.Sign, bias=K + 0.5, scale=-1.0, acc=V("acc", 0, 1))
-            halve(3)
-            tt(L("sha"), L("sh"), L("a"), Op.mult)
-            tt(L("sel"), L("sha"), L("so"), Op.max)
+            if t == 1:
+                o = p ^ STEP[0]
+                hi, lo = max(p, o), min(p, o)
+                ts(L("d%d" % hi), V("lp1"), UNIT * 4 ** hi, Op.is_ge, UNIT * 4 ** hi, Op.mult)
+                tt(digit(r), digit(r), L("wr4"), Op.add)
+                tt(L("d%d" % lo), V("lp1"), L("d%d" % hi), Op.subtract)
+                mean(1)
+                tt(L("dp"), L("d%d" % p), L("wp4"), Op.add)
+            else:
+                tt(L("dp"), L("wp4"), ahead, Op.add)
+                tt(L("pk"), L("wr4"), V("gs", 163, 240, 4), Op.add)
+                mean(1)
             mean(2)
-            tt(L("sel2"), L("sel"), L("wv"), Op.mult)
-            ts(L("cut"), V("c2"), V("acc", 0, 1), Op.is_lt)
-            tt(L("zz"), L("sel2"), L("cut"), Op.mult)
-            foffs()
+            ts(four("fa", 3), V("c2"), V("la%d" % t), Op.is_ge, -BIG, Op.mult)
             mean(3)
+            sources()
+            foffs()
+            ts(L("rc"), four("fo", 3), WDO + OFF, Op.is_ge)
+            if t == 1:
+                tt(digit(o), L("d%d" % o), L("rc"), Op.mult)
+                tt(digit(p), L("dp"), L("rc"), Op.mult)
+                send(r ^ STEP[2], V("lp2"), V("gl", 160, 240), "ap2")
+            else:
+                tt(L("pkp"), L("dp"), L("rc"), Op.mult)
+                tt(L("ov"), L("pkp"), L("pk"), Op.add)
         act(V("own"), ind(V("xh"), V(le)), Fn.Copy)
+        for bank, b in ((0, 0), (6, 2), (1, 1), (7, 3), (2, 2), (3, 3)):
+            mm("ps%d" % bank, 128, E(b)[0], E(b)[1], V(lq, 0, 128), V(ls, 0, 128))
         for b in range(4):
-            mm("ps%d" % b, 128, E(b)[0], E(b)[1], V(lq, 0, 128), V(ls, 0, 128))
-        for b in range(4):
-            act(W(t, wdh, wah, b), V("ps%d" % b, 0, A), Fn.Copy, scale=2.0)
-            tt(W(t, wah, wah + A, b), V("own", b, 4 * A, 4), V("ps%d" % b, 0, A), Op.add)
-        whole = W(t, 0, wah + A)
-        for b in range(2):
-            cp(W(t + 1, WX, WX + C, b), ind(whole, V("foff", 20 * b, 20 * b + 20)))
-            act(W(t + 1, WX, WX + C, b + 2), ind(whole, V("foff", 20 * b + 40, 20 * b + 60)), Fn.Copy)
+            act(W(t, wdh, wdh + A, b), V("ps%d" % b, 0, A), Fn.Copy, scale=2.0)
+        for bank, b in ((6, 2), (7, 3), (0, 0), (1, 1)):
+            tt(W(t, wdh + gap, wdh + gap + A, b), V("own", b, 4 * A, 4), V("ps%d" % bank, 0, A), Op.add)
 
-    quant(V("qx3"), V("sx3"), W(R, WX, WX + C))
-    mm("ps0", C, V("qv"), V("sv"), V("qx3"), V("sx3"))
+    ts(V("ovu"), L("ov"), 1.0 / UNIT, Op.mult)
+    for (lo, hi), bank in ((upper, "ps2"), (lower, "ps0")):
+        gather(R, (lo, hi))
+        pack(R, (lo, hi))
+        mm(bank, hi - lo, V("qv"), V("sv"), V("qx3", lo, hi), V("sx3", lo, hi))
     store("y", T.oc[:], V("qx3"), T.qx3[:].bitcast(dt.uint8))
+    act(V("yo", n1, C), V("ps2", 0, C - n1), Fn.Copy)
     for k in range(4):
         store("ys"[k % 2], T.osc[4 * k:4 * k + 4, :], V("sx3"), T.sx3[32 * k:32 * k + 4, :])
-    act(V("yo"), V("ps0", 0, C), Fn.Copy)
+    act(V("yo", 0, n1), V("ps0", 0, n1), Fn.Copy)
     store("s", T.y[:], V("yo"), T.yo[:])
-    ts(L("wp4"), L("a"), wp4, Op.mult)
-    ts(L("wr4"), L("wr"), wr4, Op.mult)
-    ts(L("rc"), L("zz"), 0.0, Op.is_gt)
-    tt(L("dp"), L("wp4"), V("gs", 3, 80, 4), Op.add)
-    tt(L("pk"), L("wr4"), V("gs", 163, 240, 4), Op.add)
-    tt(L("pkp"), L("dp"), L("rc"), Op.mult)
-    tt(L("ov"), L("pkp"), L("pk"), Op.add)
-    cp(V("ovu"), L("ov"))
     cp(V("ovr"), ind(V("iow"), V("ovu")))
     store("y", T.ov[:], V("ovr"), T.ovr[0:128:16, :])
 

@@ -5,7 +5,9 @@ C, A, K, R = 320, 96, 128, 3
 STEP = [1, 2, 3]
 NV = 11
 SP = 10
-MID = 18
+MID = 14
+LEAD = 5
+SHARE = False
 FIRST = "ps0"
 HV = 0
 DV = 1
@@ -46,7 +48,7 @@ _buf("m16", C, F); _buf("mask", C, B); _buf("nmask", C, B); _buf("kc", 20, F)
 _buf("c4", C, F); _buf("cval", C, F); _buf("l16", 20, F); _buf("cx", 20, F); _buf("cdo", 20, F); _buf("c2", 20, F)
 _buf("m4", 240, F); _buf("pa", A, F); _buf("pb", A, F); _buf("pat", A, F); _buf("rs", 240, B); _buf("iow", 256, B)
 _buf("mm", C, F); _buf("hd", C, F); _buf("eq", C, B); _buf("nc", C, B); _buf("ini", 20, F)
-_buf("fl", NV * C, B); _buf("cum", NV * 160, B); _buf("sg", (20 - NV) * C, B); _buf("junk", C, B)
+_buf("fl", NV * C, B); _buf("cum", NV * 160, B); _buf("sg", (21 - NV) * C, B); _buf("junk", C, B)
 _buf("sq", 80, F); _buf("so", 80, F); _buf("e", C, F); _buf("es", A, F)
 _buf("moff", 80, U); _buf("foff", 80, U); _buf("wu", 20, U); _buf("wrow", C, B); _buf("wcum", C, B)
 _buf("fa", 80, F); _buf("fb", 80, F); _buf("fo", 80, F)
@@ -218,10 +220,10 @@ def rank_program(g, core, T, topo):
     act(V("c2"), V("cx"), Fn.Identity, bias=float(-C - 2 * WX - 2 * OFF), scale=2.0)
     act(V("cval"), V("c4"), Fn.Identity, bias=tcol)
 
-    def gather(t, piece):
+    def gather(t, piece, b):
         lo, hi = piece
-        whole = W(t - 1, 0, WEND if t > 1 else WDO + 2 * A)
-        for b in range(4):
+        if t:
+            whole = W(t - 1, 0, WEND if t > 1 else WDO + 2 * A)
             o, a = W(t, WX + lo, WX + hi, b), ind(whole, V("foff", 20 * b + lo // 16, 20 * b + hi // 16))
             if b < 2:
                 cp(o, a)
@@ -231,6 +233,17 @@ def rank_program(g, core, T, topo):
     def pack(t, piece):
         lo, hi = piece
         quant(V("qx%d" % t, lo, hi), V("sx%d" % t, lo, hi), W(t, WX + lo, WX + hi))
+
+    def state(t, product, beside=None):
+        for b in range(4):
+            gather(t, upper, b)
+        gather(t, lower, 0)
+        pack(t, upper)
+        product()
+        for b in range(1, 4):
+            gather(t, lower, b)
+        if beside: beside()
+        pack(t, lower)
 
     for t in range(R):
         p = r ^ STEP[t]
@@ -256,19 +269,21 @@ def rank_program(g, core, T, topo):
 
         def count(k):
             o, n = C * (k - NV), 16 * k + 16
-            fn, b = (Fn.Sign, 0.5) if k < MID else (Fn.Relu, 0.0)
+            fn, b = (Fn.Sign, 0.5) if k >= MID else (Fn.Relu, 0.0)
             act(V("sg", o, o + n), V("sg", o, o + n), fn, bias=b, scale=-1.0 if b else 1.0, acc=V("sq", 4 * k + 1, 4 * k + 2))
             if n < C:
                 act(V("sg", o + n, o + C), V("sg", o + n, o + C), fn, bias=-b, scale=-1.0, acc=V("sq", 4 * k + 2, 4 * k + 3))
 
-        def compare(k):
+        def compare(k, between=None):
             o, n = C * k, 16 * k + 16
             ts(V("fl", o, o + n), V("ps0", 0, n), sc(k), Op.is_ge)
-            ts(V("fl", o + n, o + C), V("ps0", n, C), sc(k), Op.is_gt)
+            if between: between()
+            if not (SHARE and k == SP):
+                ts(V("fl", o + n, o + C), V("ps0", n, C), sc(k), Op.is_gt)
 
         def total(k):
-            o = C * k
-            scan(V("cum", 160 * k, 160 * k + 160), V("fl", o, o + 160), V("fl", o + 160, o + C), V("ini", k, k + 1), Op.add, Op.add)
+            o, h = C * k, 8 * k + 8 if SHARE and k == SP else 160
+            scan(V("cum", 160 * k, 160 * k + h), V("fl", o, o + h), V("fl", o + h, o + 2 * h), V("ini", k, k + 1), Op.add, Op.add)
 
         def invert(lo, hi):
             cp(ind(V("e"), V(rk, lo, hi)), V("cval", 16 * lo, 16 * hi))
@@ -277,63 +292,82 @@ def rank_program(g, core, T, topo):
             if t:
                 scaled(vector, W(t, WDO, WDH, b), V("ps%d" % (4 + b), 0, C), 2.0)
 
-        if t: gather(t, upper)
-        pack(t, upper)
-        mm("ps2", C - n1, V("qup"), V("sup"), V(qx, n1, C), V(sx, n1, C))
-        if t:
-            gather(t, lower)
-            masked(upper)
-        pack(t, lower)
+        state(t, lambda: mm("ps2", C - n1, V("qup"), V("sup"), V(qx, n1, C), V(sx, n1, C)))
         for bank in sorted(("ps0", "ps1"), key=lambda b: b != FIRST):
             mm(bank, C, V("qup"), V("sup"), V(qx), V(sx))
+        masked(upper)
         if t:
             send(p, V(lq, A, A + C), V(qx), "ao%d" % t, True)
             send(p, V(ls, A, A + C), V(sx), "ao%d" % t)
             arrive(p, [V(lq, A, A + C), V(ls, A, A + C)], "ao%d" % t)
+            if t == 1:
+                ts(L("nb"), V("pre1"), 1.0, Op.is_lt, BIG, Op.mult)
+            else:
+                arrive(p, [V("lp2")], "ap2")
+                tt(V("dd"), V("lp2"), V("gl", 160, 240), Op.subtract)
+            hold(upper)
+            if t == 2:
+                ts(V("gl", 0, 80), V("dd"), 0.0, Op.max)
+                ts(V("gl", 80, 160), V("dd"), -1.0, Op.mult, 0.0, Op.max)
+            if FIRST == "ps1": equal(upper)
+            masked(lower)
         else:
-            masked(upper)
             tt(V("pat"), V("pa"), V("pb"), Op.add)
-        hold(upper)
-        if t == 1:
-            ts(L("nb"), V("pre1"), 1.0, Op.is_lt, BIG, Op.mult)
-        equal(upper)
-        sign(NV)
-        for k in range(NV, 20):
-            if k + 1 < 20: sign(k + 1)
+            masked(lower)
+            hold(upper)
+        if SHARE:
+            o, n = C * (20 - NV), 16 * SP + 16
+            act(V("sg", o + n, o + C), V("ps1", n, C), Fn.Sign, bias=sc(SP), scale=-1.0)
+        sign(19)
+        if SHARE:
+            act(V("sg", o + n, o + C), V("sg", o + n, o + C), Fn.Relu, scale=-1.0, acc=V("sq", 4 * SP + 2, 4 * SP + 3))
+        for k in range(19, NV - 1, -1):
+            if k > NV: sign(k - 1)
             count(k)
-        rows = list(range(SP, NV)) + list(range(SP))
-        masked(lower)
-        for k in rows[:NV - SP]: compare(k)
-        hold(lower)
-        ties(upper)
-        ts(V("sq", 4 * NV, 4 * MID, 4), tie(NV, MID), 2.0, Op.mult)
-        tt(V("ini", MID, 20), tie(MID, 20), V("kc", MID, 20), Op.add)
+        if FIRST == "ps1" and t:
+            compare(SP)
+            hold(lower)
+            ties(upper)
+        else:
+            equal(upper)
+            hold(lower)
+            compare(SP)
+            ties(upper)
         compare(0)
         equal(lower)
+        ts(V("sq", 4 * MID, 80, 4), tie(MID, 20), 2.0, Op.mult)
+        tt(V("ini", NV, MID), tie(NV, MID), V("kc", NV, MID), Op.add)
         compare(1)
         ties(lower)
         compare(2)
         ts(V("ini", 0, NV), tie(0, NV), -160.0, Op.add)
-        for i, k in enumerate(rows):
-            if k + 3 + NV - SP < SP + NV - SP and k < SP: compare(k + 3)
+        for k in range(3, LEAD - 1): compare(k)
+        total(SP)
+        early = SP - LEAD + 1
+        for k in range(early - 1):
+            compare(k + LEAD - 1)
             total(k)
-        scan(V("so", 4 * NV, 4 * MID), V("rs", 4 * NV, 4 * MID), V("sq", 4 * NV, 4 * MID), 0.0, Op.mult, Op.add)
-        if t == 2:
-            arrive(p, [V("lp2")], "ap2")
-            tt(V("dd"), V("lp2"), V("gl", 160, 240), Op.subtract)
-        ts(V(rk, 0, NV), V("cum", 159, 160 * NV, 160), 160.0, Op.add)
-        ts(V(rk, NV, MID), V("so", 4 * NV + 2, 4 * MID, 4), 0.5, Op.mult, 160.0, Op.add)
-        if t == 2:
-            ts(V("gl", 0, 80), V("dd"), 0.0, Op.max)
-            ts(V("gl", 80, 160), V("dd"), -1.0, Op.mult, 0.0, Op.max)
-        invert(0, MID)
-        for k in range(MID, 20):
+        total(early - 1)
+        compare(SP - 1, lambda: ts(V(rk, 0, early), V("cum", 159, 160 * early, 160), 160.0, Op.add))
+        invert(0, early)
+        scan(V("so", 4 * MID, 80), V("rs", 4 * MID, 80), V("sq", 4 * MID, 80), 0.0, Op.mult, Op.add)
+        for k in range(early, SP):
+            total(k)
+            if k == early + 1:
+                ts(V(rk, MID, 20), V("so", 4 * MID + 2, 80, 4), 0.5, Op.mult, 160.0, Op.add)
+        invert(MID, 20)
+        if SHARE:
+            ts(V(rk, early, SP), V("cum", 160 * early + 159, 160 * SP, 160), 160.0, Op.add)
+            ts(V(rk, SP, NV), V("cum", 160 * SP + 87, 160 * SP + 88), V("sq", 4 * SP + 2, 4 * SP + 3), Op.add, 160.0, Op.add)
+        else:
+            ts(V(rk, early, NV), V("cum", 160 * early + 159, 160 * NV, 160), 160.0, Op.add)
+        for k in range(MID - 1, NV - 1, -1):
             ts(V(rk, k, k + 1), V("sq", 4 * k + 2, 4 * k + 3), V("sq", 4 * k + 1, 4 * k + 2), Op.subtract, V("ini", k, k + 1), Op.add)
         send(p, V(lr), V(rk), "ar%d" % t)
         arrive(p, [V(lr)], "ar%d" % t)
         if t == 2:
             scan(V("gs"), V("rs"), V("gl"), 0.0, Op.mult, Op.add)
-        invert(MID, 20)
+        invert(early, MID)
         if t:
             for b in range(4):
                 mm("ps%d" % (4 + b), C, E(b)[0], E(b)[1], V(lq, A, A + C), V(ls, A, A + C))
@@ -363,11 +397,23 @@ def rank_program(g, core, T, topo):
         for b in range(4):
             ts(V("moff", 20 * b, 20 * b + 20), four("fb", 3), 4.0, Op.mult, b - 4 * OFF, Op.add)
         ts(four("fa", 2), nw, 1.0, Op.is_lt, float(gap), Op.mult)
+        o = p ^ STEP[0]
+        hi, lo = max(p, o), min(p, o)
+        if t == 1:
+            arrive(p, [V("lp1")], "ap1")
+            ts(L("d%d" % hi), V("lp1"), UNIT * 4 ** hi, Op.is_ge, UNIT * 4 ** hi, Op.mult)
         if t:
+            ts(L("wr4"), V(rk), float(A), Op.is_lt, wr4, Op.mult)
             scan(V("wcum"), V("wrow"), V("wrow"), 0.0, Op.add, Op.max)
+        if t == 1:
+            tt(L("d%d" % lo), V("lp1"), L("d%d" % hi), Op.subtract)
         for b in range(4):
             act(V("rl", A * b, A * b + A), V("ps%d" % b, 0, A), Fn.Relu, scale=0.03125)
             tt(W(t, WH, WX, b), V("rl", A * b, A * b + A), V("z", b, 4 * A, 4), Op.add)
+        if t == 1:
+            tt(digit(r), digit(r), L("wr4"), Op.add)
+        if t == 2:
+            tt(L("pk"), L("wr4"), V("gs", 163, 240, 4), Op.add)
         if t:
             act(V("junk"), V("wcum"), Fn.Sign, bias=K + 0.5, scale=-1.0, acc=V("acc%d" % t))
             send(p, V("la%d" % t), V("acc%d" % t), "ac%d" % t)
@@ -407,38 +453,22 @@ def rank_program(g, core, T, topo):
             quant(V(lq, A, A + 128), V(ls, A, A + 128), W(0, WX, WX + 128))
             quant(V("qv"), V("sv"), V("vt"))
         else:
-            if t == 1:
-                arrive(p, [V("lp1")], "ap1")
             ahead = V("lp1") if t == 1 else V("gs", 3, 80, 4)
             tt(four("fb", 1), V("cdo"), ahead, Op.min)
             ts(L("wp4"), V(lr), float(A), Op.is_lt, wp4, Op.mult)
-            ts(L("wr4"), V(rk), float(A), Op.is_lt, wr4, Op.mult)
             mean(0)
-            if t == 1:
-                o = p ^ STEP[0]
-                hi, lo = max(p, o), min(p, o)
-                ts(L("d%d" % hi), V("lp1"), UNIT * 4 ** hi, Op.is_ge, UNIT * 4 ** hi, Op.mult)
-                tt(digit(r), digit(r), L("wr4"), Op.add)
-                tt(L("d%d" % lo), V("lp1"), L("d%d" % hi), Op.subtract)
-                mean(1)
-                tt(L("dp"), L("d%d" % p), L("wp4"), Op.add)
-            else:
-                tt(L("dp"), L("wp4"), ahead, Op.add)
-                tt(L("pk"), L("wr4"), V("gs", 163, 240, 4), Op.add)
-                mean(1)
-            mean(2)
+            tt(L("dp"), L("d%d" % p) if t == 1 else ahead, L("wp4"), Op.add)
+            mean(1)
             ts(four("fa", 3), V("c2"), V("la%d" % t), Op.is_ge, -BIG, Op.mult)
-            mean(3)
+            mean(2)
             sources()
-            foffs()
+            mean(3)
             ts(L("rc"), four("fo", 3), WDO + OFF, Op.is_ge)
+            foffs()
             if t == 1:
                 tt(digit(o), L("d%d" % o), L("rc"), Op.mult)
                 tt(digit(p), L("dp"), L("rc"), Op.mult)
                 send(r ^ STEP[2], V("lp2"), V("gl", 160, 240), "ap2")
-            else:
-                tt(L("pkp"), L("dp"), L("rc"), Op.mult)
-                tt(L("ov"), L("pkp"), L("pk"), Op.add)
         act(V("own"), ind(V("xh"), V(le)), Fn.Copy)
         for bank, b in ((0, 0), (6, 2), (1, 1), (7, 3), (2, 2), (3, 3)):
             mm("ps%d" % bank, 128, E(b)[0], E(b)[1], V(lq, 0, 128), V(ls, 0, 128))
@@ -446,12 +476,15 @@ def rank_program(g, core, T, topo):
             act(W(t, wdh, wdh + A, b), V("ps%d" % b, 0, A), Fn.Copy, scale=2.0)
         for bank, b in ((6, 2), (7, 3), (0, 0), (1, 1)):
             tt(W(t, wdh + gap, wdh + gap + A, b), V("own", b, 4 * A, 4), V("ps%d" % bank, 0, A), Op.add)
+        if t == 2:
+            tt(L("pkp"), L("dp"), L("rc"), Op.mult)
 
-    ts(V("ovu"), L("ov"), 1.0 / UNIT, Op.mult)
-    for (lo, hi), bank in ((upper, "ps2"), (lower, "ps0")):
-        gather(R, (lo, hi))
-        pack(R, (lo, hi))
-        mm(bank, hi - lo, V("qv"), V("sv"), V("qx3", lo, hi), V("sx3", lo, hi))
+    def upper_y():
+        mm("ps2", C - n1, V("qv"), V("sv"), V("qx3", n1, C), V("sx3", n1, C))
+        tt(L("ov"), L("pkp"), L("pk"), Op.add)
+
+    state(R, upper_y, lambda: ts(V("ovu"), L("ov"), 1.0 / UNIT, Op.mult))
+    mm("ps0", n1, V("qv"), V("sv"), V("qx3", 0, n1), V("sx3", 0, n1))
     store("y", T.oc[:], V("qx3"), T.qx3[:].bitcast(dt.uint8))
     act(V("yo", n1, C), V("ps2", 0, C - n1), Fn.Copy)
     for k in range(4):

@@ -5,14 +5,16 @@ C, A, K, R = 320, 96, 128, 3
 STEP = [1, 2, 3]
 NV = 11
 SP = 10
+SPY = 8
 MID = 14
-LEAD = 5
-SHARE = False
+EARLY = 8
+COPY = False
+SHARE = ()
 FIRST = "ps0"
-HV = 0
-DV = 1
+HV = (1, 0, 0)
+DS = 3
 WH, WX, WDO, WDH, WAO, WEND = 0, 96, 416, 736, 832, 1248
-BIG = 4096.0
+BIG, HUGE = 4096.0, 2.0 ** 40
 OFF = 1024.0
 UNIT = 2048.0
 
@@ -44,18 +46,20 @@ _buf("rl", 4 * A, F); _buf("xh", 4 * C, B); _buf("own", 4 * A, B); _buf("yo", C,
 for _b in range(8):
     _buf("ps%d" % _b, 512, F, "psum")
 _buf("pi", 4, I); _buf("pf", 8, F); _buf("oui", 8, I); _buf("ou", 8, U)
-_buf("m16", C, F); _buf("mask", C, B); _buf("nmask", C, B); _buf("kc", 20, F)
+_buf("m16", C, B); _buf("mask", C, B); _buf("nmask", C, B); _buf("kc", 20, F)
 _buf("c4", C, F); _buf("cval", C, F); _buf("l16", 20, F); _buf("cx", 20, F); _buf("cdo", 20, F); _buf("c2", 20, F)
-_buf("m4", 240, F); _buf("pa", A, F); _buf("pb", A, F); _buf("pat", A, F); _buf("rs", 240, B); _buf("iow", 256, B)
-_buf("mm", C, F); _buf("hd", C, F); _buf("eq", C, B); _buf("nc", C, B); _buf("ini", 20, F)
-_buf("fl", NV * C, B); _buf("cum", NV * 160, B); _buf("sg", (21 - NV) * C, B); _buf("junk", C, B)
+_buf("m4", 240, B); _buf("pa", A, F); _buf("pb", A, F); _buf("pat", A, F); _buf("rs", 240, B); _buf("iow", 256, B)
+_buf("sr", C, F); _buf("mm", C, F); _buf("hd", C, F); _buf("eq", C, B); _buf("nc", C, B); _buf("ini", 20, F)
+RW = C // 2 + 2
+SCRATCH["fl"] = ("sbuf", [128, 2, NV * RW], B); _buf("cum", NV * RW, B)
+_buf("sg", 20 * C, B); _buf("junk", C, B)
 _buf("sq", 80, F); _buf("so", 80, F); _buf("e", C, F); _buf("es", A, F)
 _buf("moff", 80, U); _buf("foff", 80, U); _buf("wu", 20, U); _buf("wrow", C, B); _buf("wcum", C, B)
 _buf("fa", 80, F); _buf("fb", 80, F); _buf("fo", 80, F)
 _buf("sm", 24 * 20, F)
 _buf("dd", 80, B); _buf("gl", 240, B); _buf("gs", 240, B); _buf("ovu", 20, U); _buf("ovr", C, F)
 
-SEMAPHORES = ["cv", "cs", "ct", "cg", "lx", "lu", "lw", "lws", "lv", "out", "sent", "ap1", "ap2", "ao1", "ao2", "ac1", "ac2"] + \
+SEMAPHORES = ["cv", "cs", "ct", "cg", "lx", "lxl", "lu", "lw", "lws", "lv", "out", "sent", "ap1", "ap2", "ao1", "ao2", "ac1", "ac2"] + \
     ["%s%d" % (n, t) for t in range(R) for n in ("ae", "ar", "ah")]
 
 
@@ -73,6 +77,11 @@ def rank_program(g, core, T, topo):
         cols = np.arange(n) if name.startswith("ps") else np.arange(lo, hi, step)
         return {"ap": ap, "at": [(name, cols)], "also": []}
 
+    def flags(half, lo, hi, step=1):
+        ap = T.fl[:, :, lo:hi] if half is None else T.fl[:, half, lo:hi:step]
+        cols = np.concatenate([NV * RW * h + np.arange(lo, hi, step) for h in ((0, 1) if half is None else (half,))])
+        return {"ap": ap, "at": [("fl", cols)], "also": []}
+
     def ind(win, off, words=False):
         ap = win["ap"].bitcast(dt.uint32) if words else win["ap"]
         return {"ap": ap.indirect(off["ap"]), "at": win["at"], "also": off["at"]}
@@ -88,7 +97,7 @@ def rank_program(g, core, T, topo):
         deps = set()
         for name, cols in rd + wr:
             if name not in last_w:
-                last_w[name] = np.full(SCRATCH[name][1][1], -1)
+                last_w[name] = np.full(int(np.prod(SCRATCH[name][1][1:])), -1)
                 last_r[name] = {}
             deps.update(int(d) for d in np.unique(last_w[name][cols]))
         for name, cols in wr + [a for a in rd if a[0].startswith("ps")]:
@@ -97,7 +106,7 @@ def rank_program(g, core, T, topo):
                     deps.update(int(d) for d in np.unique(a[cols]))
         deps.discard(-1)
         for name, cols in rd:
-            last_r[name].setdefault(stream, np.full(SCRATCH[name][1][1], -1))[cols] = me
+            last_r[name].setdefault(stream, np.full(len(last_w[name]), -1))[cols] = me
         for name, cols in wr:
             last_w[name][cols] = me
         seq[stream] = seq.get(stream, -1) + 1
@@ -176,8 +185,9 @@ def rank_program(g, core, T, topo):
     n1 = 16 * SP
     upper, lower = (n1, C), (0, n1)
 
-    load("y", W(0, WX, WX + C), W(0, WX, WX + C)["ap"], T.x[:], "lx")
-    load("s", V("ut"), T.ut[:], T.u[:], "lu")
+    load("y", V("ut"), T.ut[:], T.u[:], "lu")
+    for (lo, hi), q, sem in ((upper, "s", "lx"), (lower, "y", "lxl")):
+        load(q, W(0, WX + lo, WX + hi), W(0, WX + lo, WX + hi)["ap"], T.x[:, 4 * lo:4 * hi], sem)
     load("y", V("qw"), T.qw[:].bitcast(dt.uint8), T.wc[:], "lw", [W(0, WX, WX + C)])
     load("y", V("sw"), T.sw[:], T.ws[:], "lws")
     load("y", V("vt"), T.vt[:], T.v[:], "lv")
@@ -192,6 +202,9 @@ def rank_program(g, core, T, topo):
     ms(V("half"), 0.5)
     ms(V("z", 4 * A, 512), 0.0)
     ms(V("sq"), 0.0)
+    ms(flags(0, 0, NV * RW, RW), HUGE)
+    ms(flags(0, RW - 1, NV * RW, RW), 0.0)
+    ms(flags(1, RW - 1, NV * RW, RW), -HUGE)
     ms(V("fa"), 0.0)
     ms(V("fb"), 0.0)
     ts(V("pi", 1, 2), V("pi", 0, 1), 15, Op.bitwise_and)
@@ -206,13 +219,11 @@ def rank_program(g, core, T, topo):
     ts(mulcol, qcol, 3.0, Op.is_equal, 2.0 ** -13, Op.max)
     ts(V("mask"), V("m16"), lcol, Op.is_equal)
     ts(V("nmask"), V("m16"), lcol, Op.not_equal)
-    ts(V("pa"), V("m4", 0, A), qcol, Op.not_equal)
-    ts(V("pb"), V("m4", 0, A), q1col, Op.is_equal, 8191.0, Op.mult)
-    ts(V("rs"), V("m4"), 0.0, Op.not_equal)
     for b in range(4):
         o = V("et", 512 * b, 512 * b + 512)
         add("g", lambda o=o, b=b: g.affine_select(o["ap"], T.half[:], [[1, 512]], Op.is_equal, 0.0, -b, -4), [V("half")], [o])
     quant(V("qu"), V("su"), V("ut"))
+    quant(V("qx0", n1, C), V("sx0", n1, C), W(0, WX + n1, WX + C))
     add("v", lambda: g.vector.tensor_copy(T.qup[:].bitcast(dt.uint32), ind(V("qu"), V("ou"), True)["ap"]), [V("qu"), V("ou")], [V("qup")])
     act(V("sup"), ind(V("su"), V("ou")), Fn.Copy)
     act(V("cx"), V("l16"), Fn.Identity, bias=lcol)
@@ -234,11 +245,11 @@ def rank_program(g, core, T, topo):
         lo, hi = piece
         quant(V("qx%d" % t, lo, hi), V("sx%d" % t, lo, hi), W(t, WX + lo, WX + hi))
 
-    def state(t, product, beside=None):
+    def state(t, product, beside=None, upper=upper, lower=lower):
         for b in range(4):
             gather(t, upper, b)
         gather(t, lower, 0)
-        pack(t, upper)
+        if t: pack(t, upper)
         product()
         for b in range(1, 4):
             gather(t, lower, b)
@@ -264,26 +275,27 @@ def rank_program(g, core, T, topo):
             return V("hd", 16 * k + 15, 16 * k + 16)
 
         def sign(k):
-            o = C * (k - NV)
-            act(V("sg", o, o + C), V("ps1", 0, C), Fn.Sign, bias=sc(k), scale=-1.0)
+            o, n = C * k, 16 * k + 16 if k in SHARE else 0
+            act(V("sg", o + n, o + C), V("ps1", n, C), Fn.Sign, bias=sc(k), scale=-1.0)
 
         def count(k):
-            o, n = C * (k - NV), 16 * k + 16
+            o, n = C * k, 16 * k + 16
             fn, b = (Fn.Sign, 0.5) if k >= MID else (Fn.Relu, 0.0)
-            act(V("sg", o, o + n), V("sg", o, o + n), fn, bias=b, scale=-1.0 if b else 1.0, acc=V("sq", 4 * k + 1, 4 * k + 2))
+            if k not in SHARE:
+                act(V("sg", o, o + n), V("sg", o, o + n), fn, bias=b, scale=-1.0 if b else 1.0, acc=V("sq", 4 * k + 1, 4 * k + 2))
             if n < C:
                 act(V("sg", o + n, o + C), V("sg", o + n, o + C), fn, bias=-b, scale=-1.0, acc=V("sq", 4 * k + 2, 4 * k + 3))
 
         def compare(k, between=None):
-            o, n = C * k, 16 * k + 16
-            ts(V("fl", o, o + n), V("ps0", 0, n), sc(k), Op.is_ge)
+            o, n = RW * k + 1, 16 * k + 16
+            ts(flags(None, o, o + n // 2), V("ps0", 0, n), sc(k), Op.is_ge)
             if between: between()
-            if not (SHARE and k == SP):
-                ts(V("fl", o + n, o + C), V("ps0", n, C), sc(k), Op.is_gt)
+            if k not in SHARE:
+                ts(flags(None, o + n // 2, o + C // 2), V("ps0", n, C), sc(k), Op.is_gt)
 
-        def total(k):
-            o, h = C * k, 8 * k + 8 if SHARE and k == SP else 160
-            scan(V("cum", 160 * k, 160 * k + h), V("fl", o, o + h), V("fl", o + h, o + 2 * h), V("ini", k, k + 1), Op.add, Op.add)
+        def total(lo, hi):
+            o, n = RW * lo, RW * hi - (152 - 8 * lo if lo in SHARE else 0) - 1
+            scan(V("cum", o, n), flags(0, o, n), flags(1, o, n), -HUGE, Op.add, Op.add)
 
         def invert(lo, hi):
             cp(ind(V("e"), V(rk, lo, hi)), V("cval", 16 * lo, 16 * hi))
@@ -292,9 +304,15 @@ def rank_program(g, core, T, topo):
             if t:
                 scaled(vector, W(t, WDO, WDH, b), V("ps%d" % (4 + b), 0, C), 2.0)
 
-        state(t, lambda: mm("ps2", C - n1, V("qup"), V("sup"), V(qx, n1, C), V(sx, n1, C)))
+        state(t, lambda: [mm(bank, C - n1, V("qup"), V("sup"), V(qx, n1, C), V(sx, n1, C)) for bank in ("ps2", "ps3")[:1 + COPY]])
         for bank in sorted(("ps0", "ps1"), key=lambda b: b != FIRST):
             mm(bank, C, V("qup"), V("sup"), V(qx), V(sx))
+        if COPY:
+            act(V("sr", n1, C), V("ps3", 0, C - n1), Fn.Copy)
+            act(V("sr", 0, n1), V("ps1", 0, n1), Fn.Copy)
+        if t == 0:
+            ts(V("pa"), V("m4", 0, A), qcol, Op.not_equal)
+            ts(V("pb"), V("m4", 0, A), q1col, Op.is_equal, 8191.0, Op.mult)
         masked(upper)
         if t:
             send(p, V(lq, A, A + C), V(qx), "ao%d" % t, True)
@@ -315,15 +333,8 @@ def rank_program(g, core, T, topo):
             tt(V("pat"), V("pa"), V("pb"), Op.add)
             masked(lower)
             hold(upper)
-        if SHARE:
-            o, n = C * (20 - NV), 16 * SP + 16
-            act(V("sg", o + n, o + C), V("ps1", n, C), Fn.Sign, bias=sc(SP), scale=-1.0)
-        sign(19)
-        if SHARE:
-            act(V("sg", o + n, o + C), V("sg", o + n, o + C), Fn.Relu, scale=-1.0, acc=V("sq", 4 * SP + 2, 4 * SP + 3))
-        for k in range(19, NV - 1, -1):
-            if k > NV: sign(k - 1)
-            count(k)
+            ts(V("rs"), V("m4"), 0.0, Op.not_equal)
+        srows = [k for k in SHARE if k >= SP] + list(range(19, MID - 1, -1)) + [k for k in SHARE if k < SP] + list(range(MID - 1, NV - 1, -1))
         if FIRST == "ps1" and t:
             compare(SP)
             hold(lower)
@@ -333,6 +344,11 @@ def rank_program(g, core, T, topo):
             hold(lower)
             compare(SP)
             ties(upper)
+        sign(srows[0])
+        for k, nxt in zip(srows, srows[1:] + [None]):
+            if nxt is not None: sign(nxt)
+            count(k)
+        for k in range(SP + 1, NV): compare(k)
         compare(0)
         equal(lower)
         ts(V("sq", 4 * MID, 80, 4), tie(MID, 20), 2.0, Op.mult)
@@ -340,27 +356,22 @@ def rank_program(g, core, T, topo):
         compare(1)
         ties(lower)
         compare(2)
-        ts(V("ini", 0, NV), tie(0, NV), -160.0, Op.add)
-        for k in range(3, LEAD - 1): compare(k)
-        total(SP)
-        early = SP - LEAD + 1
-        for k in range(early - 1):
-            compare(k + LEAD - 1)
-            total(k)
-        total(early - 1)
-        compare(SP - 1, lambda: ts(V(rk, 0, early), V("cum", 159, 160 * early, 160), 160.0, Op.add))
-        invert(0, early)
+        ts(flags(1, 0, NV * RW, RW), tie(0, NV), -160.0, Op.add)
+        early = EARLY
+        for k in range(3, SP - 1):
+            compare(k)
+            if k == 3 and SHARE: total(SP, NV)
+        total(0, early)
+        compare(SP - 1, lambda: ts(V(rk, 0, early), V("cum", RW - 2, RW * early, RW), 160.0, Op.add))
         scan(V("so", 4 * MID, 80), V("rs", 4 * MID, 80), V("sq", 4 * MID, 80), 0.0, Op.mult, Op.add)
-        for k in range(early, SP):
-            total(k)
-            if k == early + 1:
-                ts(V(rk, MID, 20), V("so", 4 * MID + 2, 80, 4), 0.5, Op.mult, 160.0, Op.add)
+        invert(0, early)
+        ts(V(rk, MID, 20), V("so", 4 * MID + 2, 80, 4), 0.5, Op.mult, 160.0, Op.add)
+        last = SP if SHARE else NV
+        total(early, last)
         invert(MID, 20)
-        if SHARE:
-            ts(V(rk, early, SP), V("cum", 160 * early + 159, 160 * SP, 160), 160.0, Op.add)
-            ts(V(rk, SP, NV), V("cum", 160 * SP + 87, 160 * SP + 88), V("sq", 4 * SP + 2, 4 * SP + 3), Op.add, 160.0, Op.add)
-        else:
-            ts(V(rk, early, NV), V("cum", 160 * early + 159, 160 * NV, 160), 160.0, Op.add)
+        ts(V(rk, early, last), V("cum", RW * early + RW - 2, RW * last, RW), 160.0, Op.add)
+        for k in SHARE:
+            ts(V(rk, k, k + 1), V("cum", RW * k + 8 * k + 8, RW * k + 8 * k + 9), V("sq", 4 * k + 2, 4 * k + 3), Op.add, 160.0, Op.add)
         for k in range(MID - 1, NV - 1, -1):
             ts(V(rk, k, k + 1), V("sq", 4 * k + 2, 4 * k + 3), V("sq", 4 * k + 1, 4 * k + 2), Op.subtract, V("ini", k, k + 1), Op.add)
         send(p, V(lr), V(rk), "ar%d" % t)
@@ -371,15 +382,21 @@ def rank_program(g, core, T, topo):
         if t:
             for b in range(4):
                 mm("ps%d" % (4 + b), C, E(b)[0], E(b)[1], V(lq, A, A + C), V(ls, A, A + C))
-        dold(0); dold(1)
+        for b in range(DS): dold(b)
+
+        def unit(b):
+            if t == 0:
+                quant(E(b)[0], E(b)[1], V("et", 512 * b, 512 * b + 512))
+
         ts(L("u"), V(rk), float(A), Op.is_ge, BIG, Op.mult)
         if t == 2:
             ts(L("nb"), V("gs", 83, 160, 4), 1.0, Op.is_lt, BIG, Op.mult)
+        ts(L("rk"), V(rk), OFF, Op.add)
         scan(V("es"), V("pat"), V("e", 0, A), 0.0, Op.mult, Op.add)
         nw = L("nw") if t else L("u")
         if t:
             tt(nw, L("u"), L("nb"), Op.min)
-        ts(L("rk"), V(rk), OFF, Op.add)
+        unit(1)
         ts(V(eo), V("es", 3, A, 4), mulcol, Op.mult)
         if t:
             ts(V("wu"), nw, 1.0, Op.is_lt)
@@ -396,36 +413,28 @@ def rank_program(g, core, T, topo):
             act(V("wrow"), ind(V("iow"), V("wu")), Fn.Copy)
         for b in range(4):
             ts(V("moff", 20 * b, 20 * b + 20), four("fb", 3), 4.0, Op.mult, b - 4 * OFF, Op.add)
-        ts(four("fa", 2), nw, 1.0, Op.is_lt, float(gap), Op.mult)
+        unit(3)
+        unit(2)
         o = p ^ STEP[0]
         hi, lo = max(p, o), min(p, o)
-        if t == 1:
-            arrive(p, [V("lp1")], "ap1")
-            ts(L("d%d" % hi), V("lp1"), UNIT * 4 ** hi, Op.is_ge, UNIT * 4 ** hi, Op.mult)
         if t:
-            ts(L("wr4"), V(rk), float(A), Op.is_lt, wr4, Op.mult)
             scan(V("wcum"), V("wrow"), V("wrow"), 0.0, Op.add, Op.max)
-        if t == 1:
-            tt(L("d%d" % lo), V("lp1"), L("d%d" % hi), Op.subtract)
         for b in range(4):
             act(V("rl", A * b, A * b + A), V("ps%d" % b, 0, A), Fn.Relu, scale=0.03125)
             tt(W(t, WH, WX, b), V("rl", A * b, A * b + A), V("z", b, 4 * A, 4), Op.add)
-        if t == 1:
-            tt(digit(r), digit(r), L("wr4"), Op.add)
-        if t == 2:
-            tt(L("pk"), L("wr4"), V("gs", 163, 240, 4), Op.add)
+        ts(four("fa", 2), nw, 1.0, Op.is_lt, float(gap), Op.mult)
         if t:
             act(V("junk"), V("wcum"), Fn.Sign, bias=K + 0.5, scale=-1.0, acc=V("acc%d" % t))
             send(p, V("la%d" % t), V("acc%d" % t), "ac%d" % t)
             arrive(p, [V("la%d" % t)], "ac%d" % t)
-        dold(2)
+        for b in range(DS, 4): dold(b)
         quant(V("qh%d" % t), V("sh%d" % t), W(t, 0, 128))
         send(p, V(lq, 0, A), V("qh%d" % t, 0, A), "ah%d" % t, True)
         send(p, V(ls, 0, A), V("sh%d" % t, 0, A), "ah%d" % t)
         arrive(p, [V(lq, 0, A), V(ls, 0, A)], "ah%d" % t)
 
         def halve(b):
-            scaled(b < HV, V("xh", b, 4 * C, 4), ind(W(t, 0, WX + C), V("moff", 20 * b, 20 * b + 20)), 0.5)
+            scaled(b < HV[t], V("xh", b, 4 * C, 4), ind(W(t, 0, WX + C), V("moff", 20 * b, 20 * b + 20)), 0.5)
 
         def mean(b):
             tt(W(t, WAO, WAO + C, b), V("xh", b, 4 * C, 4), V("ps%d" % (4 + b), 0, C), Op.add)
@@ -439,7 +448,6 @@ def rank_program(g, core, T, topo):
 
         for b in range(4):
             halve(b)
-        dold(3, DV)
         ts(four("fa", 1), V(lr), wdh + OFF, Op.add)
         ts(four("fb", 0), V(lr), float(A), Op.is_ge, -BIG, Op.mult)
         if t == 0:
@@ -449,15 +457,25 @@ def rank_program(g, core, T, topo):
             tt(V("pre1"), digit(r), digit(p), Op.add)
             foffs()
             send(r ^ STEP[1], V("lp1"), V("pre1"), "ap1")
-            quant(V("qe"), V("se"), V("et"))
+            unit(0)
             quant(V(lq, A, A + 128), V(ls, A, A + 128), W(0, WX, WX + 128))
             quant(V("qv"), V("sv"), V("vt"))
         else:
+            if t == 1:
+                arrive(p, [V("lp1")], "ap1")
+                ts(L("d%d" % hi), V("lp1"), UNIT * 4 ** hi, Op.is_ge, UNIT * 4 ** hi, Op.mult)
             ahead = V("lp1") if t == 1 else V("gs", 3, 80, 4)
             tt(four("fb", 1), V("cdo"), ahead, Op.min)
             ts(L("wp4"), V(lr), float(A), Op.is_lt, wp4, Op.mult)
+            ts(L("wr4"), V(rk), float(A), Op.is_lt, wr4, Op.mult)
+            if t == 1:
+                tt(L("d%d" % lo), V("lp1"), L("d%d" % hi), Op.subtract)
             mean(0)
             tt(L("dp"), L("d%d" % p) if t == 1 else ahead, L("wp4"), Op.add)
+            if t == 1:
+                tt(digit(r), digit(r), L("wr4"), Op.add)
+            else:
+                tt(L("pk"), L("wr4"), V("gs", 163, 240, 4), Op.add)
             mean(1)
             ts(four("fa", 3), V("c2"), V("la%d" % t), Op.is_ge, -BIG, Op.mult)
             mean(2)
@@ -479,18 +497,22 @@ def rank_program(g, core, T, topo):
         if t == 2:
             tt(L("pkp"), L("dp"), L("rc"), Op.mult)
 
+    n2 = 16 * SPY
+
     def upper_y():
-        mm("ps2", C - n1, V("qv"), V("sv"), V("qx3", n1, C), V("sx3", n1, C))
+        mm("ps2", C - n2, V("qv"), V("sv"), V("qx3", n2, C), V("sx3", n2, C))
+        store("y", T.oc[:, 4 * n2:4 * C], V("qx3", n2, C), T.qx3[:, n2:C].bitcast(dt.uint8))
         tt(L("ov"), L("pkp"), L("pk"), Op.add)
 
-    state(R, upper_y, lambda: ts(V("ovu"), L("ov"), 1.0 / UNIT, Op.mult))
-    mm("ps0", n1, V("qv"), V("sv"), V("qx3", 0, n1), V("sx3", 0, n1))
-    store("y", T.oc[:], V("qx3"), T.qx3[:].bitcast(dt.uint8))
-    act(V("yo", n1, C), V("ps2", 0, C - n1), Fn.Copy)
+    state(R, upper_y, lambda: ts(V("ovu"), L("ov"), 1.0 / UNIT, Op.mult), (n2, C), (0, n2))
+    mm("ps0", n2, V("qv"), V("sv"), V("qx3", 0, n2), V("sx3", 0, n2))
+    act(V("yo", n2, C), V("ps2", 0, C - n2), Fn.Copy)
+    store("s", T.y[:, n2:C], V("yo", n2, C), T.yo[:, n2:C])
+    store("y", T.oc[:, 0:4 * n2], V("qx3", 0, n2), T.qx3[:, 0:n2].bitcast(dt.uint8))
+    act(V("yo", 0, n2), V("ps0", 0, n2), Fn.Copy)
+    store("s", T.y[:, 0:n2], V("yo", 0, n2), T.yo[:, 0:n2])
     for k in range(4):
-        store("ys"[k % 2], T.osc[4 * k:4 * k + 4, :], V("sx3"), T.sx3[32 * k:32 * k + 4, :])
-    act(V("yo", 0, n1), V("ps0", 0, n1), Fn.Copy)
-    store("s", T.y[:], V("yo"), T.yo[:])
+        store("yyys"[k], T.osc[4 * k:4 * k + 4, :], V("sx3"), T.sx3[32 * k:32 * k + 4, :])
     cp(V("ovr"), ind(V("iow"), V("ovu")))
     store("y", T.ov[:], V("ovr"), T.ovr[0:128:16, :])
 

import numpy as np
from concourse.mybir import dt, AluOpType as Op, ActivationFunctionType as Fn

C, A, K, R = 320, 96, 128, 3
STEP = [1, 2, 3]
NV = 11
SP = 10
SPY = 8
MID = 14
EARLY = 8
COPY = False
SHARE = ()
FIRST = "ps0"
HV = (1, 0, 0)
DS = 3
WH, WX, WDO, WDH, WAO, WEND = 0, 96, 416, 736, 832, 1248
BIG, HUGE = 4096.0, 2.0 ** 40
OFF = 1024.0
UNIT = 2048.0

F, B, U, I, Q, S = "float32", "bfloat16", "uint16", "int32", "float8_e4m3fn_x4", "uint8"
SCRATCH = {}


def _buf(name, n, d, where="sbuf"):
    SCRATCH[name] = (where, [128, n], d)


for _t in range(R):
    _buf("win%d" % _t, 4 * WEND, B)
    _buf("qx%d" % _t, C, Q); _buf("sx%d" % _t, C, S)
    _buf("qh%d" % _t, 128, Q); _buf("sh%d" % _t, 128, S)
    _buf("lq%d" % _t, A + C, Q); _buf("ls%d" % _t, A + C, S)
    _buf("eo%d" % _t, 24, U); _buf("le%d" % _t, 24, U); _buf("rk%d" % _t, 20, U); _buf("lr%d" % _t, 20, U)
_buf("win3", 4 * (WX + C), B); _buf("qx3", C, Q); _buf("sx3", C, S)
_buf("pre1", 20, B); _buf("lp1", 20, B); _buf("lp2", 80, B)
for _t in (1, 2):
    _buf("acc%d" % _t, 1, F); _buf("la%d" % _t, 1, F)
for _n in "uv":
    _buf(_n + "t", 512, B); _buf("q" + _n, 128, Q); _buf("s" + _n, 128, S)
_buf("qup", 128, Q); _buf("sup", 128, S)
_buf("qw", 512, Q); _buf("sw", 512, S)
_buf("half", 512, B); _buf("et", 2048, B); _buf("qe", 512, Q); _buf("se", 512, S)
_buf("z", 512, B); _buf("qz", 128, Q); _buf("sz", 128, S)
_buf("rl", 4 * A, F); _buf("xh", 4 * C, B); _buf("own", 4 * A, B); _buf("yo", C, F)
for _b in range(8):
    _buf("ps%d" % _b, 512, F, "psum")
_buf("pi", 4, I); _buf("pf", 8, F); _buf("oui", 8, I); _buf("ou", 8, U)
_buf("m16", C, B); _buf("mask", C, B); _buf("nmask", C, B); _buf("kc", 20, F)
_buf("c4", C, F); _buf("cval", C, F); _buf("l16", 20, F); _buf("cx", 20, F); _buf("cdo", 20, F); _buf("c2", 20, F)
_buf("m4", 240, B); _buf("pa", A, F); _buf("pb", A, F); _buf("pat", A, F); _buf("rs", 240, B); _buf("iow", 256, B)
_buf("sr", C, F); _buf("mm", C, F); _buf("hd", C, F); _buf("eq", C, B); _buf("nc", C, B); _buf("ini", 20, F)
RW = C // 2 + 2
SCRATCH["fl"] = ("sbuf", [128, 2, NV * RW], B); _buf("cum", NV * RW, B)
_buf("sg", 20 * C, B); _buf("junk", C, B)
_buf("sq", 80, F); _buf("so", 80, F); _buf("e", C, F); _buf("es", A, F)
_buf("moff", 80, U); _buf("foff", 80, U); _buf("wu", 20, U); _buf("wrow", C, B); _buf("wcum", C, B)
_buf("fa", 80, F); _buf("fb", 80, F); _buf("fo", 80, F)
_buf("sm", 24 * 20, F)
_buf("dd", 80, B); _buf("gl", 240, B); _buf("gs", 240, B); _buf("ovu", 20, U); _buf("ovr", C, F)

SEMAPHORES = ["cv", "cs", "ct", "cg", "lx", "lxl", "lu", "lw", "lws", "lv", "out", "sent", "ap1", "ap2", "ao1", "ao2", "ac1", "ac2"] + \
    ["%s%d" % (n, t) for t in range(R) for n in ("ae", "ar", "ah")]


def rank_program(g, core, T, topo):
    r = T.rank_of(core)
    if r is None:
        return
    queues = {"v": g.vector, "s": g.scalar, "t": g.tensor, "g": g, "y": g.sync}
    ops, last_w, last_r, seq, sent, stored = [], {}, {}, {}, [0], [0]

    def V(name, lo=0, hi=None, step=1):
        n = SCRATCH[name][1][1]
        hi = n if hi is None else hi
        ap = T[name][:, lo:hi] if step == 1 else T[name][:, lo:hi:step]
        cols = np.arange(n) if name.startswith("ps") else np.arange(lo, hi, step)
        return {"ap": ap, "at": [(name, cols)], "also": []}

    def flags(half, lo, hi, step=1):
        ap = T.fl[:, :, lo:hi] if half is None else T.fl[:, half, lo:hi:step]
        cols = np.concatenate([NV * RW * h + np.arange(lo, hi, step) for h in ((0, 1) if half is None else (half,))])
        return {"ap": ap, "at": [("fl", cols)], "also": []}

    def ind(win, off, words=False):
        ap = win["ap"].bitcast(dt.uint32) if words else win["ap"]
        return {"ap": ap.indirect(off["ap"]), "at": win["at"], "also": off["at"]}

    def ap(x):
        return x["ap"] if isinstance(x, dict) else x

    def add(q, fn, reads, writes, stream=None, token=None):
        me = len(ops)
        stream = stream or q
        rd = [a for x in reads if isinstance(x, dict) for a in x["at"] + x["also"]] + [a for x in writes for a in x["also"]]
        wr = [a for x in writes for a in x["at"]]
        deps = set()
        for name, cols in rd + wr:
            if name not in last_w:
                last_w[name] = np.full(int(np.prod(SCRATCH[name][1][1:])), -1)
                last_r[name] = {}
            deps.update(int(d) for d in np.unique(last_w[name][cols]))
        for name, cols in wr + [a for a in rd if a[0].startswith("ps")]:
            for s, a in last_r[name].items():
                if s != stream:
                    deps.update(int(d) for d in np.unique(a[cols]))
        deps.discard(-1)
        for name, cols in rd:
            last_r[name].setdefault(stream, np.full(len(last_w[name]), -1))[cols] = me
        for name, cols in wr:
            last_w[name][cols] = me
        seq[stream] = seq.get(stream, -1) + 1
        ops.append({"q": q, "fn": fn, "deps": deps, "stream": stream, "seq": seq[stream], "token": token, "waits": [], "need": False})

    def tt(o, a, b, op): add("v", lambda: g.vector.tensor_tensor(ap(o), ap(a), ap(b), op), [a, b], [o])
    def cp(o, a): add("v", lambda: g.vector.tensor_copy(ap(o), ap(a)), [a], [o])
    def ms(o, c): add("v", lambda: g.vector.memset(ap(o), c), [], [o])
    def scan(o, a, b, ini, o0, o1): add("v", lambda: g.vector.tensor_tensor_scan(ap(o), ap(a), ap(b), ap(ini), o0, o1), [a, b, ini], [o])
    def quant(q, s, a): add("v", lambda: g.vector.quantize_mx(ap(q), ap(s), ap(a)), [a], [q, s])

    def ts(o, a, s1, o0, s2=None, o1=None):
        if o1 is None:
            add("v", lambda: g.vector.tensor_scalar(ap(o), ap(a), ap(s1), None, o0), [a, s1], [o])
        else:
            add("v", lambda: g.vector.tensor_scalar(ap(o), ap(a), ap(s1), ap(s2), o0, o1), [a, s1, s2], [o])

    def act(o, a, fn, bias=None, scale=None, acc=None):
        kw = {}
        if bias is not None: kw["bias"] = ap(bias)
        if scale is not None: kw["scale"] = ap(scale)
        if acc is not None: kw["accum_out"] = ap(acc)
        add("s", lambda: g.scalar.activation(ap(o), ap(a), fn, **kw), [a, bias, scale], [o] + ([acc] if acc else []))

    def scaled(vector, o, a, c):
        if vector:
            ts(o, a, c, Op.mult)
        else:
            act(o, a, Fn.Copy, scale=c)

    def mm(o, n, lq, ls, rq, rs):
        add("t", lambda: g.tensor.matmul_mx(T[o][:, 0:n], ap(lq), ap(ls), ap(rq), ap(rs), True, True), [lq, ls, rq, rs], [V(o)])

    def iota(o, pat, base, cm=0, flag=True):
        if flag:
            add("g", lambda: g.iota(ap(o), pat, base, cm, allow_small_or_imprecise_dtypes=True), [], [o])
        else:
            add("g", lambda: g.iota(ap(o), pat, base, cm), [], [o])

    def load(q, o, oap, src, sem, after=()):
        add(q, lambda: queues[q].dma_start(oap, src).then_inc(T.sem[sem], 16), list(after), [o], stream=sem, token=(sem, 16))

    def store(q, dst, a, aap):
        stored[0] += 16
        add(q, lambda: queues[q].dma_start(dst, aap).then_inc(T.sem.out, 16), [a], [], stream="st%d" % stored[0], token=("out", 0))

    def send(peer, o, a, sem, codes=False):
        dst = T.cores[peer]
        rid, pid = topo.addr(dst)[0:2]
        sent[0] += len(topo.engines(core, dst))
        oa, aa = (o["ap"].bitcast(dt.uint8), a["ap"].bitcast(dt.uint8)) if codes else (o["ap"], a["ap"])
        add("g", lambda: g.remote_dma(oa, aa, T.sem[sem], T.sem.sent, pid, rid, topo.mask(core, dst)), [a], [],
            stream="rd%d" % sent[0], token=("sent", 0))

    def arrive(peer, views, sem):
        add(None, None, [], views, stream=sem, token=(sem, len(views) * len(topo.engines(T.cores[peer], core))))

    slots = {}

    def L(name):
        k = slots.setdefault(name, len(slots))
        return V("sm", 20 * k, 20 * k + 20)

    def W(t, lo, hi, b=None):
        return V("win%d" % t, 4 * lo, 4 * hi) if b is None else V("win%d" % t, 4 * lo + b, 4 * hi, 4)

    def digit(i):
        return V("gl", 160 + i, 240, 4)

    def four(name, i):
        return V(name, i, 80, 4)

    def E(b):
        return V("qe", 128 * b, 128 * b + 128), V("se", 128 * b, 128 * b + 128)

    n1 = 16 * SP
    upper, lower = (n1, C), (0, n1)

    load("y", V("ut"), T.ut[:], T.u[:], "lu")
    for (lo, hi), q, sem in ((upper, "s", "lx"), (lower, "y", "lxl")):
        load(q, W(0, WX + lo, WX + hi), W(0, WX + lo, WX + hi)["ap"], T.x[:, 4 * lo:4 * hi], sem)
    load("y", V("qw"), T.qw[:].bitcast(dt.uint8), T.wc[:], "lw", [W(0, WX, WX + C)])
    load("y", V("sw"), T.sw[:], T.ws[:], "lws")
    load("y", V("vt"), T.vt[:], T.v[:], "lv")
    iota(V("pi", 0, 1), [[0, 1]], 0, 1, False)
    iota(V("oui"), [[16, 8]], 0, 0, False)
    iota(V("m16"), [[0, 20], [1, 16]], 0)
    iota(V("m4"), [[0, 60], [1, 4]], 0)
    iota(V("kc"), [[16, 20]], 16)
    iota(V("l16"), [[16, 20]], WX + int(OFF))
    iota(V("c4"), [[4, C]], 0)
    iota(V("iow"), [[1, 256]], 0)
    ms(V("half"), 0.5)
    ms(V("z", 4 * A, 512), 0.0)
    ms(V("sq"), 0.0)
    ms(flags(0, 0, NV * RW, RW), HUGE)
    ms(flags(0, RW - 1, NV * RW, RW), 0.0)
    ms(flags(1, RW - 1, NV * RW, RW), -HUGE)
    ms(V("fa"), 0.0)
    ms(V("fb"), 0.0)
    ts(V("pi", 1, 2), V("pi", 0, 1), 15, Op.bitwise_and)
    ts(V("pi", 2, 3), V("pi", 0, 1), 3, Op.bitwise_and)
    ts(V("pi", 3, 4), V("pi", 0, 1), 2, Op.logical_shift_right, 3, Op.bitwise_and)
    cp(V("ou"), V("oui"))
    ms(four("fa", 0), -4 * BIG)
    ms(four("fb", 2), -4 * BIG)
    cp(V("pf", 0, 3), V("pi", 1, 4))
    lcol, tcol, qcol, q1col, mulcol = [V("pf", i, i + 1) for i in range(5)]
    ts(q1col, qcol, 1.0, Op.add)
    ts(mulcol, qcol, 3.0, Op.is_equal, 2.0 ** -13, Op.max)
    ts(V("mask"), V("m16"), lcol, Op.is_equal)
    ts(V("nmask"), V("m16"), lcol, Op.not_equal)
    for b in range(4):
        o = V("et", 512 * b, 512 * b + 512)
        add("g", lambda o=o, b=b: g.affine_select(o["ap"], T.half[:], [[1, 512]], Op.is_equal, 0.0, -b, -4), [V("half")], [o])
    quant(V("qu"), V("su"), V("ut"))
    quant(V("qx0", n1, C), V("sx0", n1, C), W(0, WX + n1, WX + C))
    add("v", lambda: g.vector.tensor_copy(T.qup[:].bitcast(dt.uint32), ind(V("qu"), V("ou"), True)["ap"]), [V("qu"), V("ou")], [V("qup")])
    act(V("sup"), ind(V("su"), V("ou")), Fn.Copy)
    act(V("cx"), V("l16"), Fn.Identity, bias=lcol)
    act(V("cdo"), V("cx"), Fn.Identity, bias=float(WDO - WX))
    act(V("c2"), V("cx"), Fn.Identity, bias=float(-C - 2 * WX - 2 * OFF), scale=2.0)
    act(V("cval"), V("c4"), Fn.Identity, bias=tcol)

    def gather(t, piece, b):
        lo, hi = piece
        if t:
            whole = W(t - 1, 0, WEND if t > 1 else WDO + 2 * A)
            o, a = W(t, WX + lo, WX + hi, b), ind(whole, V("foff", 20 * b + lo // 16, 20 * b + hi // 16))
            if b < 2:
                cp(o, a)
            else:
                act(o, a, Fn.Copy)

    def pack(t, piece):
        lo, hi = piece
        quant(V("qx%d" % t, lo, hi), V("sx%d" % t, lo, hi), W(t, WX + lo, WX + hi))

    def state(t, product, beside=None, upper=upper, lower=lower):
        for b in range(4):
            gather(t, upper, b)
        gather(t, lower, 0)
        if t: pack(t, upper)
        product()
        for b in range(1, 4):
            gather(t, lower, b)
        if beside: beside()
        pack(t, lower)

    for t in range(R):
        p = r ^ STEP[t]
        qx, sx, lq, ls, eo, le, rk, lr = ["%s%d" % (n, t) for n in ("qx", "sx", "lq", "ls", "eo", "le", "rk", "lr")]
        wdh, gap = (WDH, WAO - WDO) if t else (WDO, A)
        wr4, wp4 = UNIT * 4 ** r, UNIT * 4 ** p
        scores = {upper: V("ps2", 0, C - n1), lower: V("ps0", 0, n1)}

        def masked(piece): tt(V("mm", *piece), scores[piece], V("mask", *piece), Op.mult)
        def hold(piece): scan(V("hd", *piece), V("nmask", *piece), V("mm", *piece), 0.0, Op.mult, Op.add)
        def equal(piece): tt(V("eq", *piece), scores[piece], V("hd", *piece), Op.is_equal)
        def ties(piece): scan(V("nc", *piece), V("nmask", *piece), V("eq", *piece), 0.0, Op.mult, Op.subtract)

        def tie(lo, hi):
            return V("nc", 16 * lo + 15, 16 * hi, 16)

        def sc(k):
            return V("hd", 16 * k + 15, 16 * k + 16)

        def sign(k):
            o, n = C * k, 16 * k + 16 if k in SHARE else 0
            act(V("sg", o + n, o + C), V("ps1", n, C), Fn.Sign, bias=sc(k), scale=-1.0)

        def count(k):
            o, n = C * k, 16 * k + 16
            fn, b = (Fn.Sign, 0.5) if k >= MID else (Fn.Relu, 0.0)
            if k not in SHARE:
                act(V("sg", o, o + n), V("sg", o, o + n), fn, bias=b, scale=-1.0 if b else 1.0, acc=V("sq", 4 * k + 1, 4 * k + 2))
            if n < C:
                act(V("sg", o + n, o + C), V("sg", o + n, o + C), fn, bias=-b, scale=-1.0, acc=V("sq", 4 * k + 2, 4 * k + 3))

        def compare(k, between=None):
            o, n = RW * k + 1, 16 * k + 16
            ts(flags(None, o, o + n // 2), V("ps0", 0, n), sc(k), Op.is_ge)
            if between: between()
            if k not in SHARE:
                ts(flags(None, o + n // 2, o + C // 2), V("ps0", n, C), sc(k), Op.is_gt)

        def total(lo, hi):
            o, n = RW * lo, RW * hi - (152 - 8 * lo if lo in SHARE else 0) - 1
            scan(V("cum", o, n), flags(0, o, n), flags(1, o, n), -HUGE, Op.add, Op.add)

        def invert(lo, hi):
            cp(ind(V("e"), V(rk, lo, hi)), V("cval", 16 * lo, 16 * hi))

        def dold(b, vector=False):
            if t:
                scaled(vector, W(t, WDO, WDH, b), V("ps%d" % (4 + b), 0, C), 2.0)

        state(t, lambda: [mm(bank, C - n1, V("qup"), V("sup"), V(qx, n1, C), V(sx, n1, C)) for bank in ("ps2", "ps3")[:1 + COPY]])
        for bank in sorted(("ps0", "ps1"), key=lambda b: b != FIRST):
            mm(bank, C, V("qup"), V("sup"), V(qx), V(sx))
        if COPY:
            act(V("sr", n1, C), V("ps3", 0, C - n1), Fn.Copy)
            act(V("sr", 0, n1), V("ps1", 0, n1), Fn.Copy)
        if t == 0:
            ts(V("pa"), V("m4", 0, A), qcol, Op.not_equal)
            ts(V("pb"), V("m4", 0, A), q1col, Op.is_equal, 8191.0, Op.mult)
        masked(upper)
        if t:
            send(p, V(lq, A, A + C), V(qx), "ao%d" % t, True)
            send(p, V(ls, A, A + C), V(sx), "ao%d" % t)
            arrive(p, [V(lq, A, A + C), V(ls, A, A + C)], "ao%d" % t)
            if t == 1:
                ts(L("nb"), V("pre1"), 1.0, Op.is_lt, BIG, Op.mult)
            else:
                arrive(p, [V("lp2")], "ap2")
                tt(V("dd"), V("lp2"), V("gl", 160, 240), Op.subtract)
            hold(upper)
            if t == 2:
                ts(V("gl", 0, 80), V("dd"), 0.0, Op.max)
                ts(V("gl", 80, 160), V("dd"), -1.0, Op.mult, 0.0, Op.max)
            if FIRST == "ps1": equal(upper)
            masked(lower)
        else:
            tt(V("pat"), V("pa"), V("pb"), Op.add)
            masked(lower)
            hold(upper)
            ts(V("rs"), V("m4"), 0.0, Op.not_equal)
        srows = [k for k in SHARE if k >= SP] + list(range(19, MID - 1, -1)) + [k for k in SHARE if k < SP] + list(range(MID - 1, NV - 1, -1))
        if FIRST == "ps1" and t:
            compare(SP)
            hold(lower)
            ties(upper)
        else:
            equal(upper)
            hold(lower)
            compare(SP)
            ties(upper)
        sign(srows[0])
        for k, nxt in zip(srows, srows[1:] + [None]):
            if nxt is not None: sign(nxt)
            count(k)
        for k in range(SP + 1, NV): compare(k)
        compare(0)
        equal(lower)
        ts(V("sq", 4 * MID, 80, 4), tie(MID, 20), 2.0, Op.mult)
        tt(V("ini", NV, MID), tie(NV, MID), V("kc", NV, MID), Op.add)
        compare(1)
        ties(lower)
        compare(2)
        ts(flags(1, 0, NV * RW, RW), tie(0, NV), -160.0, Op.add)
        early = EARLY
        for k in range(3, SP - 1):
            compare(k)
            if k == 3 and SHARE: total(SP, NV)
        total(0, early)
        compare(SP - 1, lambda: ts(V(rk, 0, early), V("cum", RW - 2, RW * early, RW), 160.0, Op.add))
        scan(V("so", 4 * MID, 80), V("rs", 4 * MID, 80), V("sq", 4 * MID, 80), 0.0, Op.mult, Op.add)
        invert(0, early)
        ts(V(rk, MID, 20), V("so", 4 * MID + 2, 80, 4), 0.5, Op.mult, 160.0, Op.add)
        last = SP if SHARE else NV
        total(early, last)
        invert(MID, 20)
        ts(V(rk, early, last), V("cum", RW * early + RW - 2, RW * last, RW), 160.0, Op.add)
        for k in SHARE:
            ts(V(rk, k, k + 1), V("cum", RW * k + 8 * k + 8, RW * k + 8 * k + 9), V("sq", 4 * k + 2, 4 * k + 3), Op.add, 160.0, Op.add)
        for k in range(MID - 1, NV - 1, -1):
            ts(V(rk, k, k + 1), V("sq", 4 * k + 2, 4 * k + 3), V("sq", 4 * k + 1, 4 * k + 2), Op.subtract, V("ini", k, k + 1), Op.add)
        send(p, V(lr), V(rk), "ar%d" % t)
        arrive(p, [V(lr)], "ar%d" % t)
        if t == 2:
            scan(V("gs"), V("rs"), V("gl"), 0.0, Op.mult, Op.add)
        invert(early, MID)
        if t:
            for b in range(4):
                mm("ps%d" % (4 + b), C, E(b)[0], E(b)[1], V(lq, A, A + C), V(ls, A, A + C))
        for b in range(DS): dold(b)

        def unit(b):
            if t == 0:
                quant(E(b)[0], E(b)[1], V("et", 512 * b, 512 * b + 512))

        ts(L("u"), V(rk), float(A), Op.is_ge, BIG, Op.mult)
        if t == 2:
            ts(L("nb"), V("gs", 83, 160, 4), 1.0, Op.is_lt, BIG, Op.mult)
        ts(L("rk"), V(rk), OFF, Op.add)
        scan(V("es"), V("pat"), V("e", 0, A), 0.0, Op.mult, Op.add)
        nw = L("nw") if t else L("u")
        if t:
            tt(nw, L("u"), L("nb"), Op.min)
        unit(1)
        ts(V(eo), V("es", 3, A, 4), mulcol, Op.mult)
        if t:
            ts(V("wu"), nw, 1.0, Op.is_lt)
        tt(L("v"), L("rk"), L("u"), Op.add)
        cp(V("z", 0, 192), ind(W(t, WX, WX + C), V(eo, 0, 12)))
        act(V("z", 192, 384), ind(W(t, WX, WX + C), V(eo, 12, 24)), Fn.Copy)
        send(p, V(le), V(eo), "ae%d" % t)
        arrive(p, [V(le)], "ae%d" % t)
        tt(four("fb", 3), L("v"), V("cx"), Op.min)
        quant(V("qz"), V("sz"), V("z"))
        for b in range(4):
            mm("ps%d" % b, 128, V("qw", 128 * b, 128 * b + 128), V("sw", 128 * b, 128 * b + 128), V("qz"), V("sz"))
        if t:
            act(V("wrow"), ind(V("iow"), V("wu")), Fn.Copy)
        for b in range(4):
            ts(V("moff", 20 * b, 20 * b + 20), four("fb", 3), 4.0, Op.mult, b - 4 * OFF, Op.add)
        unit(3)
        unit(2)
        o = p ^ STEP[0]
        hi, lo = max(p, o), min(p, o)
        if t:
            scan(V("wcum"), V("wrow"), V("wrow"), 0.0, Op.add, Op.max)
        for b in range(4):
            act(V("rl", A * b, A * b + A), V("ps%d" % b, 0, A), Fn.Relu, scale=0.03125)
            tt(W(t, WH, WX, b), V("rl", A * b, A * b + A), V("z", b, 4 * A, 4), Op.add)
        ts(four("fa", 2), nw, 1.0, Op.is_lt, float(gap), Op.mult)
        if t:
            act(V("junk"), V("wcum"), Fn.Sign, bias=K + 0.5, scale=-1.0, acc=V("acc%d" % t))
            send(p, V("la%d" % t), V("acc%d" % t), "ac%d" % t)
            arrive(p, [V("la%d" % t)], "ac%d" % t)
        for b in range(DS, 4): dold(b)
        quant(V("qh%d" % t), V("sh%d" % t), W(t, 0, 128))
        send(p, V(lq, 0, A), V("qh%d" % t, 0, A), "ah%d" % t, True)
        send(p, V(ls, 0, A), V("sh%d" % t, 0, A), "ah%d" % t)
        arrive(p, [V(lq, 0, A), V(ls, 0, A)], "ah%d" % t)

        def halve(b):
            scaled(b < HV[t], V("xh", b, 4 * C, 4), ind(W(t, 0, WX + C), V("moff", 20 * b, 20 * b + 20)), 0.5)

        def mean(b):
            tt(W(t, WAO, WAO + C, b), V("xh", b, 4 * C, 4), V("ps%d" % (4 + b), 0, C), Op.add)

        def sources():
            scan(V("fo"), V("fa"), V("fb"), 0.0, Op.add, Op.max)

        def foffs():
            for b in range(4):
                ts(V("foff", 20 * b, 20 * b + 20), four("fo", 3), 4.0, Op.mult, b - 4 * OFF, Op.add)

        for b in range(4):
            halve(b)
        ts(four("fa", 1), V(lr), wdh + OFF, Op.add)
        ts(four("fb", 0), V(lr), float(A), Op.is_ge, -BIG, Op.mult)
        if t == 0:
            ts(digit(p), V(lr), float(A), Op.is_lt, wp4, Op.mult)
            ts(digit(r), V(rk), float(A), Op.is_lt, wr4, Op.mult)
            sources()
            tt(V("pre1"), digit(r), digit(p), Op.add)
            foffs()
            send(r ^ STEP[1], V("lp1"), V("pre1"), "ap1")
            unit(0)
            quant(V(lq, A, A + 128), V(ls, A, A + 128), W(0, WX, WX + 128))
            quant(V("qv"), V("sv"), V("vt"))
        else:
            if t == 1:
                arrive(p, [V("lp1")], "ap1")
                ts(L("d%d" % hi), V("lp1"), UNIT * 4 ** hi, Op.is_ge, UNIT * 4 ** hi, Op.mult)
            ahead = V("lp1") if t == 1 else V("gs", 3, 80, 4)
            tt(four("fb", 1), V("cdo"), ahead, Op.min)
            ts(L("wp4"), V(lr), float(A), Op.is_lt, wp4, Op.mult)
            ts(L("wr4"), V(rk), float(A), Op.is_lt, wr4, Op.mult)
            if t == 1:
                tt(L("d%d" % lo), V("lp1"), L("d%d" % hi), Op.subtract)
            mean(0)
            tt(L("dp"), L("d%d" % p) if t == 1 else ahead, L("wp4"), Op.add)
            if t == 1:
                tt(digit(r), digit(r), L("wr4"), Op.add)
            else:
                tt(L("pk"), L("wr4"), V("gs", 163, 240, 4), Op.add)
            mean(1)
            ts(four("fa", 3), V("c2"), V("la%d" % t), Op.is_ge, -BIG, Op.mult)
            mean(2)
            sources()
            mean(3)
            ts(L("rc"), four("fo", 3), WDO + OFF, Op.is_ge)
            foffs()
            if t == 1:
                tt(digit(o), L("d%d" % o), L("rc"), Op.mult)
                tt(digit(p), L("dp"), L("rc"), Op.mult)
                send(r ^ STEP[2], V("lp2"), V("gl", 160, 240), "ap2")
        act(V("own"), ind(V("xh"), V(le)), Fn.Copy)
        for bank, b in ((0, 0), (6, 2), (1, 1), (7, 3), (2, 2), (3, 3)):
            mm("ps%d" % bank, 128, E(b)[0], E(b)[1], V(lq, 0, 128), V(ls, 0, 128))
        for b in range(4):
            act(W(t, wdh, wdh + A, b), V("ps%d" % b, 0, A), Fn.Copy, scale=2.0)
        for bank, b in ((6, 2), (7, 3), (0, 0), (1, 1)):
            tt(W(t, wdh + gap, wdh + gap + A, b), V("own", b, 4 * A, 4), V("ps%d" % bank, 0, A), Op.add)
        if t == 2:
            tt(L("pkp"), L("dp"), L("rc"), Op.mult)

    n2 = 16 * SPY

    def upper_y():
        mm("ps2", C - n2, V("qv"), V("sv"), V("qx3", n2, C), V("sx3", n2, C))
        store("y", T.oc[:, 4 * n2:4 * C], V("qx3", n2, C), T.qx3[:, n2:C].bitcast(dt.uint8))
        tt(L("ov"), L("pkp"), L("pk"), Op.add)

    state(R, upper_y, lambda: ts(V("ovu"), L("ov"), 1.0 / UNIT, Op.mult), (n2, C), (0, n2))
    mm("ps0", n2, V("qv"), V("sv"), V("qx3", 0, n2), V("sx3", 0, n2))
    act(V("yo", n2, C), V("ps2", 0, C - n2), Fn.Copy)
    store("s", T.y[:, n2:C], V("yo", n2, C), T.yo[:, n2:C])
    store("y", T.oc[:, 0:4 * n2], V("qx3", 0, n2), T.qx3[:, 0:n2].bitcast(dt.uint8))
    act(V("yo", 0, n2), V("ps0", 0, n2), Fn.Copy)
    store("s", T.y[:, 0:n2], V("yo", 0, n2), T.yo[:, 0:n2])
    for k in range(4):
        store("yyys"[k], T.osc[4 * k:4 * k + 4, :], V("sx3"), T.sx3[32 * k:32 * k + 4, :])
    cp(V("ovr"), ind(V("iow"), V("ovu")))
    store("y", T.ov[:], V("ovr"), T.ovr[0:128:16, :])

    known = {q: {} for q in queues}
    for o in ops:
        if o["q"] is None:
            o["clock"] = {}
            continue
        kn = known[o["q"]]
        for d in sorted(o["deps"], reverse=True):
            e = ops[d]
            if kn.get(e["stream"], -1) >= e["seq"]:
                continue
            e["need"] = True
            o["waits"].append(e)
            kn[e["stream"]] = e["seq"]
            for s, n in e["clock"].items():
                kn[s] = max(kn.get(s, -1), n)
        o["clock"] = dict(kn)
    n = {q: 0 for q in queues}
    for o in ops:
        if o["q"] is None:
            continue
        for e in o["waits"]:
            queues[o["q"]].wait_ge(T.sem[e["token"][0]], e["token"][1])
        ins = o["fn"]()
        if o["token"] is None and o["need"]:
            n[o["q"]] += 1
            o["token"] = ("c" + o["q"], n[o["q"]])
            ins.then_inc(T.sem[o["token"][0]], 1)
    g.wait_ge(T.sem.sent, sent[0])
    g.wait_ge(T.sem.out, stored[0])
